import numpy as np
import ml_dtypes


def mxq(x, axis, fmt="e4m3"):
    dtype, down = {"e4m3": (ml_dtypes.float8_e4m3fn, 7), "e5m2": (ml_dtypes.float8_e5m2, 14)}[fmt]
    v = np.moveaxis(np.asarray(x, np.float32).astype(ml_dtypes.bfloat16).astype(np.float64), axis, -1)
    blocks = v.reshape(v.shape[:-1] + (-1, 32))
    amax = np.abs(blocks).max(-1, keepdims=True)
    byte = np.maximum(np.where(amax > 0, np.frexp(amax)[1] - 1 + 127, 0) - down, 1)
    scale = np.exp2(byte - 127.0)
    codes = (blocks / scale).astype(np.float32).astype(dtype).astype(np.float64)
    return np.moveaxis((codes * scale).reshape(v.shape), -1, axis)


WIDE = False


def mx_kscale(k):
    if not WIDE:
        return np.ones(k)
    levels = np.array([10, -10, 5, -5, 0])
    if k % 512:
        return np.exp2(np.random.permutation(np.resize(levels, k // 32))).repeat(32)
    a = np.empty((k // 512, 16))
    for p in range(k // 512):
        a[p, :8] = np.random.permutation(np.resize(levels, 8))
        for g in range(8):
            far = levels[np.abs(levels - a[p, g]) >= 10]
            a[p, g + 8] = far[np.random.randint(len(far))]
    return np.exp2(a.ravel()).repeat(32)


def f64(x):
    return np.asarray(x).astype(np.float64)


def striped(idx):
    return np.tile(idx.reshape(-1, 16).T, (8, 1)).astype(np.uint16)


def unstriped(offs):
    return offs[:16].T.reshape(-1).astype(np.int64)


E2M1 = np.array([0.0, 0.5, 1.0, 1.5, 2.0, 3.0, 4.0, 6.0, -0.0, -0.5, -1.0, -1.5, -2.0, -3.0, -4.0, -6.0])


def pack_weight(w, fmt):
    k, n = w.shape
    w = f64(np.asarray(w, np.float32).astype(ml_dtypes.bfloat16)).reshape(k // 32, 32, n)
    amax = np.abs(w).max(1)
    if fmt == "e4m3":
        byte = np.frexp(amax)[1] - 1 + 127 - 7
    else:
        mant, ex = np.frexp(amax / 6.0)
        byte = np.where(mant > 0.5, ex, ex - 1) + 127
    byte = np.clip(np.where(amax > 0, byte, 1), 1, 254)
    scaled = (w * np.exp2(127.0 - byte)[:, None, :]).reshape(k, n).astype(np.float32)
    by_word = np.ascontiguousarray(scaled.reshape(k // 512, 128, 4, n).transpose(0, 1, 3, 2))
    if fmt == "e4m3":
        words = by_word.astype(ml_dtypes.float8_e4m3fn).view(np.uint8)
    else:
        c = by_word.astype(ml_dtypes.float4_e2m1fn).view(np.uint8) & 0xF
        words = (c[..., 0::2] | (c[..., 1::2] << 4)).reshape(k // 512, 128, 2 * n)
    return np.ascontiguousarray(words), np.ascontiguousarray(byte.astype(np.uint8).reshape(k // 512, 16, n))


def unpack_weight(words, scales, fmt):
    g, _, n = scales.shape
    words = np.ascontiguousarray(words).reshape(g, 128, n, -1)
    if fmt == "e4m3":
        vals = words.view(ml_dtypes.float8_e4m3fn).astype(np.float64)
    else:
        nib = np.empty((g, 128, n, 4), np.uint8)
        nib[..., 0::2] = words & 0xF
        nib[..., 1::2] = words >> 4
        vals = E2M1[nib]
    vals = vals * np.repeat(np.exp2(scales.astype(np.float64) - 127.0), 8, axis=1)[..., None]
    return vals.transpose(0, 1, 3, 2).reshape(g * 512, n)


def gelu(v):
    return 0.5 * v * (1.0 + np.tanh(np.sqrt(2.0 / np.pi) * (v + 0.044715 * v**3)))


def bf(x):
    return np.asarray(x, np.float32).astype(ml_dtypes.bfloat16)


def planes(Y):
    n, m = Y.shape
    b = f64(bf(Y)).reshape(n // 32, 32, m)
    amax = np.abs(b).max(1)
    byte = np.clip(np.where(amax > 0, np.frexp(amax)[1] - 1 + 127 - 7, 1), 1, 254)
    codes = (b * np.exp2(127.0 - byte)[:, None, :]).reshape(n, m).astype(np.float32).astype(ml_dtypes.float8_e4m3fn).view(np.uint8)
    words = codes.reshape(n // 512, 128, 4, m).transpose(0, 1, 3, 2)
    return np.ascontiguousarray(words), np.ascontiguousarray(byte.astype(np.uint8).reshape(n // 512, 16, m))


K, H, N, T, S, T2, P = 1024, 1536, 512, 2048, 512, 1024, 512

def setup_inputs():
    n = np.random.standard_normal
    s = mx_kscale(K)[:, None]
    u = mx_kscale(H)[:, None]
    d = {}
    d["tab_words"], d["tab_scales"] = pack_weight(n((K, T)) * s, "e4m3")
    d["offs"] = striped(np.random.permutation(T)[:S])
    d["offs2"] = striped(np.random.permutation(T2)[:S])
    d["offs3"] = striped(np.random.permutation(T2)[:P])
    d["w1"] = (1.5 * n((K, H)) / K**0.5 / s).astype(np.float32)
    d["gain"] = (1.3 * np.exp(0.3 * n(H)) * u[:, 0]).astype(np.float32)
    d["wgs"] = np.exp(0.3 * n((128, S))).astype(np.float32)
    d["page0"] = (n((H, T2)) * u).astype(np.float32)
    d["bx"] = (0.6 * n(H) * u[:, 0]).astype(np.float32)
    d["w2"] = (n((H, N)) / H**0.5 / u).astype(np.float32)
    d["w3_words"], d["w3_scales"] = pack_weight(0.5 * n((H, N)) / H**0.5 / u**2, "e2m1")
    return d

def reference(tab_words, tab_scales, offs, offs2, offs3, w1, gain, wgs, page0, bx, w2, w3_words, w3_scales):
    v = unpack_weight(tab_words, tab_scales, "e4m3")[:, unstriped(offs)]
    h = f64(gain)[:, None] * np.tanh(mxq(f64(w1), 0, "e4m3").T @ v)
    page = f64(page0).copy()
    page[:, unstriped(offs2)] = np.tile(f64(wgs), (H // 128, 1)) * h
    x = page[:, unstriped(offs3)] + f64(bx)[:, None]
    xx = np.square(x)
    xq = mxq(x, 0, "e4m3")
    xxq = mxq(xx, 0, "e4m3")
    w2q = mxq(f64(w2), 0, "e4m3")
    w3 = unpack_weight(w3_words, w3_scales, "e2m1")
    y = w2q.T @ xq + w3.T @ xxq
    words, scales = planes(page)
    return y, page, words, scales

@@ -1,0 +1,441 @@
+from contextlib import ExitStack
+
+import concourse.mybir as mybir
+
+K, H, N, T, S, T2, PICK = 1024, 1536, 512, 2048, 512, 1024, 512
+FLOPS = 2 * K * H * S + 2 * 2 * H * N * PICK
+
+F32 = mybir.dt.float32
+BF16 = mybir.dt.bfloat16
+I32 = mybir.dt.int32
+U32 = mybir.dt.uint32
+U16 = mybir.dt.uint16
+U8 = mybir.dt.uint8
+FP8X4 = mybir.dt.float8_e4m3fn_x4
+FP4X4 = mybir.dt.float4_e2m1fn_x4
+ACT = mybir.ActivationFunctionType
+ALU = mybir.AluOpType
+
+P = 128
+PACK = 4
+PASS = P * PACK
+KP = K // PASS
+G = H // PASS
+TILES = G * PACK
+
+
+def tile_list_rink_patch_planner_kernel(
+    tc, tab_words, tab_scales, offs, offs2, offs3, w1, gain, wgs, page0, bx, w2, w3_words, w3_scales,
+    out_0, out_1, out_2, out_3,
+):
+    nc = tc.nc
+    with ExitStack() as ctx:
+        keep = ctx.enter_context(tc.tile_pool(name="keep", bufs=1))
+        rawp = ctx.enter_context(tc.tile_pool(name="raw", bufs=6))
+        ring = ctx.enter_context(tc.tile_pool(name="ring", bufs=2))
+        hps = ctx.enter_context(tc.psum_pool(name="hps", bufs=4))
+        yps = ctx.enter_context(tc.psum_pool(name="yps", bufs=1))
+
+        lst1 = keep.tile([P, S // 16], U16, name="lst1")
+        lst2 = keep.tile([P, S // 16], U16, name="lst2")
+        lst3 = keep.tile([P, PICK // 16], U16, name="lst3")
+        gain_t = keep.tile([P, G, PACK], F32, name="gain_t")
+        bx_t = keep.tile([P, G, PACK], F32, name="bx_t")
+        tabw = keep.tile([P, KP * T], I32, name="tabw", tag="big", align_bytes=64)
+        tabs = keep.tile([P, T], U8, name="tabs", align_bytes=64)
+        wgs_first = keep.tile([P, S], F32, name="wgs_first")
+        wgs_rest = keep.tile([P, (PACK - 1) * S], F32, name="wgs_rest")
+        pages = {}
+        w3w = keep.tile([P, G, 2 * N], U8, name="w3w", align_bytes=64)
+        w3s = keep.tile([P, G, N], U8, name="w3s", align_bytes=64)
+        vw = keep.tile([P, KP * S], U32, name="vw", align_bytes=64)
+        vs = keep.tile([P, S], U8, name="vs", align_bytes=64)
+        picked = [keep.tile([P, PACK * PICK], F32, name="picked%d" % g, align_bytes=64) for g in range(G)]
+        pscale = keep.tile([P, G * T2], U8, name="pscale", align_bytes=64)
+        ybank = [yps.tile([P, PICK], F32, name="y%d" % j) for j in range(N // P)]
+
+        def rows_of(ap, g, t):
+            return ap[g * PASS:(g + 1) * PASS, :].rearrange("(p t) m -> p t m", t=PACK)[:, t, :]
+
+        raw1 = {}
+        raw2 = {}
+
+        def load_w1(g, a):
+            raw1[g, a] = rawp.tile([P, PACK, PASS], F32, name="raw", tag="raw", align_bytes=64)
+            src = w1[a * PASS:(a + 1) * PASS, g * PASS:(g + 1) * PASS]
+            nc.sync.dma_start(out=raw1[g, a][:], in_=src.rearrange("(p j) c -> p j c", j=PACK))
+
+        def load_w2(g):
+            raw2[g] = rawp.tile([P, PACK, N], F32, name="raw", tag="raw", align_bytes=64)
+            nc.sync.dma_start(out=raw2[g][:], in_=w2[g * PASS:(g + 1) * PASS, :].rearrange("(p j) c -> p j c", j=PACK))
+
+        def load_page(i):
+            pages[i] = keep.tile([P, T2], F32, name="page", tag="page%d" % (i % 10), align_bytes=64)
+            nc.sync.dma_start(out=pages[i][:], in_=rows_of(page0, i // PACK, i % PACK))
+
+        wgs_rows = wgs.rearrange("(p t) j -> p (t j)", t=PACK)
+
+        nc.vector.memset(tabs[:].bitcast(I32), 0)
+        nc.vector.memset(w3s[:].rearrange("p g c -> p (g c)").bitcast(I32), 0)
+
+        nc.sync.dma_start(lst1[:], offs)
+        load_w1(0, 0)
+        for q in range(4):
+            nc.sync.dma_start(
+                out=tabs[32 * q:32 * q + 4 * KP, :].bitcast(I32),
+                in_=tab_scales[:, 4 * q:4 * q + 4, :].bitcast(I32),
+            )
+        load_w1(0, 1)
+        for a in range(KP):
+            nc.sync.dma_start(
+                out=tabw[:, a * T:(a + 1) * T],
+                in_=tab_words[a].rearrange("p t i -> p (t i)").bitcast(I32),
+            )
+        for q in range(4):
+            nc.sync.dma_start(out=wgs_first[32 * q:32 * q + 32, :], in_=wgs_rows[:, 0:S])
+        nc.sync.dma_start(out=gain_t[:], in_=gain.rearrange("(g p t) -> p g t", g=G, t=PACK))
+        nc.sync.dma_start(lst2[:], offs2)
+        load_page(0)
+        for q in range(4):
+            nc.sync.dma_start(out=wgs_rest[32 * q:32 * q + 32, :], in_=wgs_rows[:, S:PACK * S])
+
+        def load_w3():
+            nc.sync.dma_start(out=w3w[:].bitcast(I32), in_=w3_words.rearrange("a p c -> p a c").bitcast(I32))
+            for q in range(4):
+                nc.sync.dma_start(
+                    out=w3s[32 * q:32 * q + 4, :, :].bitcast(I32),
+                    in_=w3_scales[:, 4 * q:4 * q + 4, :].rearrange("a r c -> r a c").bitcast(I32),
+                )
+
+        def load_bx():
+            nc.sync.dma_start(out=bx_t[:], in_=bx.rearrange("(g p t) -> p g t", g=G, t=PACK))
+
+        def after_scatter(i, n, dtype=U32):
+            return keep.tile([P, n * PASS], dtype, name="codes", tag="gw%d" % i, align_bytes=64)
+
+        def quantize(src, name, codes):
+            scales = keep.tile([P, PASS], U8, name=name + "s", align_bytes=64)
+            nc.vector.quantize_mx(out=codes.bitcast(FP8X4), scales=scales[:], in_=src[:])
+            return codes, scales
+
+        def walk_out(dst):
+            return dst.rearrange("p (c i t) -> p c t i", i=4, t=PACK)
+
+        def walk_in(src):
+            return src.rearrange("p (t c i) -> p c t i", i=4, t=PACK)
+
+        w1q = {}
+        w2q = {}
+
+        def prep_w1(g, a, codes):
+            wb = ring.tile([P, PASS * PACK], BF16, name="wb", tag="wb", bufs=3, align_bytes=64)
+            nc.scalar.copy(
+                out=wb[:].rearrange("p (t m j) -> p m j t", t=PACK, j=PACK),
+                in_=raw1[g, a][:].rearrange("p j (m t) -> p m j t", t=PACK),
+            )
+            w1q[g, a] = quantize(wb, "w1q%d%d" % (g, a), codes)
+
+        def prep_w2(g, codes):
+            wb = ring.tile([P, N * PACK], BF16, name="wb", tag="wb", bufs=3, align_bytes=64)
+            nc.scalar.copy(out=walk_out(wb[:]), in_=walk_in(raw2[g][:].rearrange("p j c -> p (j c)")))
+            w2q[g] = quantize(wb, "w2q%d" % g, codes)
+
+        def slot(i):
+            return picked[i // PACK][:, (i % PACK) * PICK:(i % PACK + 1) * PICK]
+
+        gw = {}
+        th = {}
+
+        def th_place(i):
+            if i == 9:
+                return slot(11)
+            if i == 10:
+                return keep.tile([P, S], F32, name="th10", tag="first_codes", align_bytes=64)[:]
+            if i == 11:
+                return picked[2][:, PICK + PICK // 2:2 * PICK + PICK // 2]
+            return slot(i)
+
+        def features(i):
+            g, t = divmod(i, PACK)
+            acc = hps.tile([P, S], F32, name="acc", tag="acc")
+            for a in range(KP):
+                codes, scales = w1q[g, a]
+                nc.tensor.matmul_mx(
+                    out=acc[:],
+                    lhsT=codes[:, t * P:(t + 1) * P].bitcast(FP8X4),
+                    lhsT_scale=scales[:, t * P:(t + 1) * P],
+                    rhs=vw[:, a * S:(a + 1) * S].bitcast(FP8X4),
+                    rhs_scale=vs[4 * a:P, :],
+                    start=(a == 0),
+                    stop=(a == KP - 1),
+                )
+            th[i] = th_place(i)
+            nc.scalar.activation(out=th[i], in_=acc[:], func=ACT.Tanh)
+
+        def factor(i):
+            g, t = divmod(i, PACK)
+            gw[i] = keep.tile([P, S], F32, name="gw", tag="gw%d" % i, align_bytes=64)
+            src = wgs_rest[:, (t - 1) * S:t * S]
+            nc.scalar.activation(out=gw[i][:], in_=src, func=ACT.Copy, scale=gain_t[:, g, t:t + 1])
+
+        def factor_first(g):
+            gw[g * PACK] = keep.tile([P, S], F32, name="gw", tag="gw%d" % (g * PACK), align_bytes=64)
+            nc.vector.tensor_scalar(gw[g * PACK][:], wgs_first[:], gain_t[:, g, 0:1], None, ALU.mult)
+
+        def rewrite(i):
+            scatter(i)
+            gather(i)
+
+        def scatter(i):
+            nc.vector.tensor_tensor(pages[i][:].indirect(lst2[:]), th[i], gw[i][:], ALU.mult)
+
+        def gather(i):
+            nc.vector.tensor_copy(slot(i), pages[i][:].indirect(lst3[:]))
+
+        def store_page(i):
+            nc.sync.dma_start(out=rows_of(out_1, i // PACK, i % PACK), in_=pages[i][:])
+
+        def bias(i):
+            g, t = divmod(i, PACK)
+            nc.scalar.activation(out=slot(i), in_=slot(i), func=ACT.Identity, bias=bx_t[:, g, t:t + 1])
+
+        xq = {}
+        xxq = {}
+
+        def cast_x(g, xb, copy):
+            copy(out=walk_out(xb), in_=walk_in(picked[g][:]))
+
+        def cast_xx(g, xxb):
+            nc.scalar.activation(out=walk_out(xxb), in_=walk_in(picked[g][:]), func=ACT.Square)
+
+        def prep_x(g, xcodes, xxcodes):
+            xb = ring.tile([P, PICK * PACK], BF16, name="xb", tag="xb", bufs=1, align_bytes=64)
+            xxb = ring.tile([P, PICK * PACK], BF16, name="xxb", tag="xxb", bufs=1, align_bytes=64)
+            cast_x(g, xb[:], nc.scalar.copy)
+            cast_xx(g, xxb[:])
+            return (lambda: xq.update({g: quantize(xb, "xq%d" % g, xcodes)}), lambda: xxq.update({g: quantize(xxb, "xxq%d" % g, xxcodes)}))
+
+        def second(g):
+            xc, xs = xq[g]
+            xxc, xxs = xxq[g]
+            wc, ws = w2q[g]
+            for j in range(N // P):
+                nc.tensor.matmul_mx(
+                    out=ybank[j][:],
+                    lhsT=wc[:, j * P:(j + 1) * P].bitcast(FP8X4),
+                    lhsT_scale=ws[:, j * P:(j + 1) * P],
+                    rhs=xc.bitcast(FP8X4),
+                    rhs_scale=xs[:],
+                    start=(g == 0),
+                    stop=False,
+                )
+            for j in range(N // P):
+                nc.tensor.matmul_mx(
+                    out=ybank[j][:],
+                    lhsT=w3w[:, g, 2 * j * P:2 * (j + 1) * P].bitcast(FP4X4),
+                    lhsT_scale=w3s[:, g, j * P:(j + 1) * P],
+                    rhs=xxc.bitcast(FP8X4),
+                    rhs_scale=xxs[:],
+                    start=False,
+                    stop=(g == G - 1),
+                )
+
+        joined = {}
+
+        def regroup(i):
+            g, t = divmod(i, PACK)
+            if t == 0:
+                joined[g] = keep.tile([P, PACK * T2], F32, name="joined", tag="big", align_bytes=64)
+            nc.sync.dma_start(out=joined[g][:, t * T2:(t + 1) * T2], in_=pages[i][:])
+
+        def narrow(i):
+            g, t = divmod(i, PACK)
+            if t == 0:
+                joined[g] = rawp.tile([P, PACK * T2], BF16, name="raw", tag="raw", align_bytes=64)
+            nc.scalar.copy(out=joined[g][:, t * T2:(t + 1) * T2], in_=pages[i][:])
+
+        pbs = {}
+
+        def cast_planes(g, u, copy=nc.scalar.copy, into=None):
+            half = T2 // 2
+            src = joined[g][:].rearrange("p (t u c i) -> p u c t i", t=PACK, u=2, i=4)
+            if into is None:
+                into = ring.tile([P, half * PACK], BF16, name="pb", tag="pb", align_bytes=64)[:]
+            pbs[g, u] = into
+            copy(out=walk_out(into), in_=src[:, u])
+
+        def quantize_planes(g, u, codes):
+            half = T2 // 2
+            nc.vector.quantize_mx(
+                out=codes[:, u * half:(u + 1) * half].bitcast(FP8X4),
+                scales=pscale[:, g * T2 + u * half:g * T2 + (u + 1) * half],
+                in_=pbs[g, u],
+            )
+
+        def planes(g, u, codes):
+            cast_planes(g, u)
+            quantize_planes(g, u, codes)
+
+        def store_codes(g, codes):
+            nc.sync.dma_start(out=out_2[g].rearrange("p m t -> p (m t)").bitcast(I32), in_=codes[:])
+
+        def part(tile, k):
+            return tile[:, k * PASS:(k + 1) * PASS]
+
+        nc.vector.tensor_copy(vs[:], tabs[:].indirect(lst1[:]))
+        first_codes = keep.tile([P, KP * PASS], U32, name="first_codes", align_bytes=64)
+        prep_w1(0, 0, part(first_codes, 0))
+        prep_w1(0, 1, part(first_codes, 1))
+        for a in range(KP):
+            nc.vector.tensor_copy(vw[:, a * S:(a + 1) * S], tabw[:, a * T:(a + 1) * T].bitcast(U32).indirect(lst1[:]))
+        for g in range(G):
+            factor_first(g)
+        load_page(1)
+        nc.sync.dma_start(lst3[:], offs3)
+        load_w1(1, 0)
+        load_w1(1, 1)
+        load_page(2)
+        load_bx()
+        load_w1(2, 0)
+        load_w1(2, 1)
+        load_page(3)
+        load_w2(0)
+        load_page(4)
+        load_w3()
+        features(0)
+        factor(1)
+        features(1)
+        features(2)
+        features(3)
+        factor(2)
+        factor(3)
+        factor(5)
+        factor(6)
+        factor(7)
+        factor(9)
+        factor(10)
+        factor(11)
+        rewrite(0)
+        rewrite(1)
+        prep_w1(1, 0, after_scatter(1, 1)[:])
+        rewrite(2)
+        prep_w1(1, 1, after_scatter(2, 1)[:])
+        bias(0)
+        bias(1)
+        bias(2)
+        features(4)
+        features(5)
+        features(6)
+        features(7)
+        rewrite(3)
+        rewrite(4)
+        regroup(0)
+        regroup(1)
+        load_page(5)
+        regroup(2)
+        regroup(3)
+        load_w2(1)
+        load_page(6)
+        load_w2(2)
+        load_page(7)
+        load_page(8)
+        load_page(9)
+        store_page(0)
+        store_page(1)
+        store_page(2)
+        store_page(3)
+        c4 = after_scatter(4, 2)
+        prep_w1(2, 0, part(c4, 0))
+        prep_w1(2, 1, part(c4, 1))
+        bias(3)
+        rewrite(5)
+        c5 = after_scatter(5, 3)
+        prep_w2(0, part(c5, 0))
+        q0 = prep_x(0, part(c5, 1), part(c5, 2))
+        q0[0]()
+        q0[1]()
+        second(0)
+        bias(4)
+        features(8)
+        features(9)
+        features(10)
+        features(11)
+        bias(5)
+        rewrite(6)
+        rewrite(7)
+        c7 = after_scatter(7, 2, I32)
+        planes(0, 0, c7)
+        planes(0, 1, c7)
+        bias(6)
+        rewrite(8)
+        regroup(4)
+        regroup(5)
+        regroup(6)
+        regroup(7)
+        load_page(10)
+        load_page(11)
+        store_page(4)
+        store_page(5)
+        store_page(6)
+        store_page(7)
+        store_codes(0, c7)
+        prep_w2(1, after_scatter(8, 1)[:])
+        bias(7)
+        scatter(9)
+        scatter(10)
+        prep_w2(2, after_scatter(9, 1)[:])
+        scatter(11)
+        c11 = after_scatter(11, 2)
+        q1 = prep_x(1, part(c11, 0), part(c11, 1))
+        bias(8)
+        narrow(8)
+        narrow(9)
+        c10 = after_scatter(10, 2, I32)
+        planes(1, 0, c10)
+        planes(1, 1, c10)
+        narrow(10)
+        narrow(11)
+        store_page(8)
+        store_page(9)
+        store_page(10)
+        store_page(11)
+        store_codes(1, c10)
+        gather(9)
+        gather(10)
+        q1[0]()
+        gather(11)
+        q1[1]()
+        second(1)
+        cast_planes(2, 0)
+        bias(9)
+        bias(10)
+        bias(11)
+        last = rawp.tile([P, 2 * PICK * PACK], BF16, name="raw", tag="raw", align_bytes=64)
+        xb2 = last[:, 0:PICK * PACK]
+        xxb2 = last[:, PICK * PACK:2 * PICK * PACK]
+        cast_xx(2, xxb2)
+        cast_x(2, xb2, nc.vector.tensor_copy)
+        c12 = keep.tile([P, T2], I32, name="last_planes", align_bytes=64)
+        c13 = keep.tile([P, 2 * PASS], U32, name="last_codes", align_bytes=64)
+        quantize_planes(2, 0, c12)
+        xq[2] = quantize(xb2, "xq2", part(c13, 0))
+        xxq[2] = quantize(xxb2, "xxq2", part(c13, 1))
+        second(2)
+        cast_planes(2, 1, nc.vector.tensor_copy, xxb2)
+        quantize_planes(2, 1, c12)
+        store_codes(2, c12)
+
+        for q in range(4):
+            nc.sync.dma_start(
+                out=out_3[:, 4 * q:4 * q + 4, :].rearrange("g r m -> r g m").bitcast(I32),
+                in_=pscale[32 * q:32 * q + 4, :].rearrange("p (g m) -> p g m", g=G).bitcast(I32),
+            )
+        yo = rawp.tile([P, N // P, PICK], F32, name="raw", tag="raw", align_bytes=64)
+        for j in range(N // P):
+            if j < N // P - 1:
+                nc.scalar.copy(out=yo[:, j, :], in_=ybank[j][:])
+            else:
+                nc.vector.tensor_copy(out=yo[:, j, :], in_=ybank[j][:])
+            if j % 2 == 1:
+                dst = out_0[(j - 1) * P:(j + 1) * P, :].rearrange("(b p) m -> p b m", b=2)
+                nc.sync.dma_start(out=dst, in_=yo[:, j - 1:j + 1, :])

@@ -1,6 +1,7 @@
 from contextlib import ExitStack
 
 import concourse.mybir as mybir
+from concourse.masks import make_identity
 
 K, H, N, T, S, T2, PICK = 1024, 1536, 512, 2048, 512, 1024, 512
 FLOPS = 2 * K * H * S + 2 * 2 * H * N * PICK
@@ -33,7 +34,7 @@ def tile_list_rink_patch_planner_kernel(
         keep = ctx.enter_context(tc.tile_pool(name="keep", bufs=1))
         rawp = ctx.enter_context(tc.tile_pool(name="raw", bufs=6))
         ring = ctx.enter_context(tc.tile_pool(name="ring", bufs=2))
-        hps = ctx.enter_context(tc.psum_pool(name="hps", bufs=4))
+        hps = ctx.enter_context(tc.psum_pool(name="hps", bufs=3))
         yps = ctx.enter_context(tc.psum_pool(name="yps", bufs=1))
 
         lst1 = keep.tile([P, S // 16], U16, name="lst1")
@@ -43,8 +44,10 @@ def tile_list_rink_patch_planner_kernel(
         bx_t = keep.tile([P, G, PACK], F32, name="bx_t")
         tabw = keep.tile([P, KP * T], I32, name="tabw", tag="big", align_bytes=64)
         tabs = keep.tile([P, T], U8, name="tabs", align_bytes=64)
-        wgs_first = keep.tile([P, S], F32, name="wgs_first")
-        wgs_rest = keep.tile([P, (PACK - 1) * S], F32, name="wgs_rest")
+        wgs_t = keep.tile([P, S], F32, name="wgs_t")
+        col_pairs = [ring.tile([P, 2 * S], F32, name="cols", tag="pb", align_bytes=64) for u in range(2)]
+        wgs_cols = [col_pairs[t // 2][:, (t % 2) * S:(t % 2 + 1) * S] for t in range(PACK)]
+        ident = keep.tile([P, P], F32, name="ident")
         pages = {}
         w3w = keep.tile([P, G, 2 * N], U8, name="w3w", align_bytes=64)
         w3s = keep.tile([P, G, N], U8, name="w3s", align_bytes=64)
@@ -52,7 +55,6 @@ def tile_list_rink_patch_planner_kernel(
         vs = keep.tile([P, S], U8, name="vs", align_bytes=64)
         picked = [keep.tile([P, PACK * PICK], F32, name="picked%d" % g, align_bytes=64) for g in range(G)]
         pscale = keep.tile([P, G * T2], U8, name="pscale", align_bytes=64)
-        ybank = [yps.tile([P, PICK], F32, name="y%d" % j) for j in range(N // P)]
 
         def rows_of(ap, g, t):
             return ap[g * PASS:(g + 1) * PASS, :].rearrange("(p t) m -> p t m", t=PACK)[:, t, :]
@@ -73,34 +75,33 @@ def tile_list_rink_patch_planner_kernel(
             pages[i] = keep.tile([P, T2], F32, name="page", tag="page%d" % (i % 10), align_bytes=64)
             nc.sync.dma_start(out=pages[i][:], in_=rows_of(page0, i // PACK, i % PACK))
 
-        wgs_rows = wgs.rearrange("(p t) j -> p (t j)", t=PACK)
+        make_identity(nc, ident[:])
 
         nc.vector.memset(tabs[:].bitcast(I32), 0)
         nc.vector.memset(w3s[:].rearrange("p g c -> p (g c)").bitcast(I32), 0)
 
         nc.sync.dma_start(lst1[:], offs)
-        load_w1(0, 0)
+        nc.sync.dma_start(out=wgs_t[:], in_=wgs)
+        nc.sync.dma_start(out=gain_t[:], in_=gain.rearrange("(g p t) -> p g t", g=G, t=PACK))
         for q in range(4):
             nc.sync.dma_start(
                 out=tabs[32 * q:32 * q + 4 * KP, :].bitcast(I32),
                 in_=tab_scales[:, 4 * q:4 * q + 4, :].bitcast(I32),
             )
+        load_w1(0, 0)
         load_w1(0, 1)
         for a in range(KP):
             nc.sync.dma_start(
                 out=tabw[:, a * T:(a + 1) * T],
                 in_=tab_words[a].rearrange("p t i -> p (t i)").bitcast(I32),
             )
-        for q in range(4):
-            nc.sync.dma_start(out=wgs_first[32 * q:32 * q + 32, :], in_=wgs_rows[:, 0:S])
-        nc.sync.dma_start(out=gain_t[:], in_=gain.rearrange("(g p t) -> p g t", g=G, t=PACK))
         nc.sync.dma_start(lst2[:], offs2)
         load_page(0)
-        for q in range(4):
-            nc.sync.dma_start(out=wgs_rest[32 * q:32 * q + 32, :], in_=wgs_rows[:, S:PACK * S])
 
         def load_w3():
             nc.sync.dma_start(out=w3w[:].bitcast(I32), in_=w3_words.rearrange("a p c -> p a c").bitcast(I32))
+
+        def load_w3_scales():
             for q in range(4):
                 nc.sync.dma_start(
                     out=w3s[32 * q:32 * q + 4, :, :].bitcast(I32),
@@ -127,9 +128,9 @@ def tile_list_rink_patch_planner_kernel(
         w1q = {}
         w2q = {}
 
-        def prep_w1(g, a, codes):
+        def prep_w1(g, a, codes, copy=nc.scalar.copy):
             wb = ring.tile([P, PASS * PACK], BF16, name="wb", tag="wb", bufs=3, align_bytes=64)
-            nc.scalar.copy(
+            copy(
                 out=wb[:].rearrange("p (t m j) -> p m j t", t=PACK, j=PACK),
                 in_=raw1[g, a][:].rearrange("p j (m t) -> p m j t", t=PACK),
             )
@@ -155,39 +156,50 @@ def tile_list_rink_patch_planner_kernel(
                 return picked[2][:, PICK + PICK // 2:2 * PICK + PICK // 2]
             return slot(i)
 
-        def features(i):
+        def features(i, c0=0, c1=S):
             g, t = divmod(i, PACK)
-            acc = hps.tile([P, S], F32, name="acc", tag="acc")
+            acc = hps.tile([P, c1 - c0], F32, name="acc", tag="acc")
             for a in range(KP):
                 codes, scales = w1q[g, a]
                 nc.tensor.matmul_mx(
                     out=acc[:],
                     lhsT=codes[:, t * P:(t + 1) * P].bitcast(FP8X4),
                     lhsT_scale=scales[:, t * P:(t + 1) * P],
-                    rhs=vw[:, a * S:(a + 1) * S].bitcast(FP8X4),
-                    rhs_scale=vs[4 * a:P, :],
+                    rhs=vw[:, a * S + c0:a * S + c1].bitcast(FP8X4),
+                    rhs_scale=vs[4 * a:P, c0:c1],
                     start=(a == 0),
                     stop=(a == KP - 1),
                 )
-            th[i] = th_place(i)
-            nc.scalar.activation(out=th[i], in_=acc[:], func=ACT.Tanh)
+            if c0 == 0:
+                th[i] = th_place(i)
+            nc.scalar.activation(out=th[i][:, c0:c1], in_=acc[:], func=ACT.Tanh)
+
+        dealt = {}
+
+        def deal_wgs():
+            turned = hps.tile([P, S], F32, name="acc", tag="acc")
+            for b in range(S // P):
+                nc.tensor.transpose(turned[:, b * P:(b + 1) * P], wgs_t[:, b * P:(b + 1) * P], ident[:])
+            rows = turned[:].rearrange("j (b p t) -> j t b p", b=S // P, t=PACK)
+            for t in range(PACK):
+                src = rows[:, t].unsqueeze(2).to_broadcast([P, S // P, 4, 32])
+                nc.scalar.copy(out=wgs_cols[t].rearrange("j (b q p) -> j b q p", b=S // P, q=4), in_=src)
+                dealt[t] = yps.tile([P, S], F32, name="dealt", tag="y%d" % t)
+                for b in range(S // P):
+                    nc.tensor.transpose(dealt[t][:, b * P:(b + 1) * P], wgs_cols[t][:, b * P:(b + 1) * P], ident[:])
 
         def factor(i):
             g, t = divmod(i, PACK)
             gw[i] = keep.tile([P, S], F32, name="gw", tag="gw%d" % i, align_bytes=64)
-            src = wgs_rest[:, (t - 1) * S:t * S]
-            nc.scalar.activation(out=gw[i][:], in_=src, func=ACT.Copy, scale=gain_t[:, g, t:t + 1])
-
-        def factor_first(g):
-            gw[g * PACK] = keep.tile([P, S], F32, name="gw", tag="gw%d" % (g * PACK), align_bytes=64)
-            nc.vector.tensor_scalar(gw[g * PACK][:], wgs_first[:], gain_t[:, g, 0:1], None, ALU.mult)
+            nc.scalar.activation(out=gw[i][:], in_=dealt[t][:], func=ACT.Copy, scale=gain_t[:, g, t:t + 1])
 
         def rewrite(i):
             scatter(i)
             gather(i)
 
-        def scatter(i):
-            nc.vector.tensor_tensor(pages[i][:].indirect(lst2[:]), th[i], gw[i][:], ALU.mult)
+        def scatter(i, c0=0, c1=S):
+            places = lst2[:, c0 // 16:c1 // 16]
+            nc.vector.tensor_tensor(pages[i][:].indirect(places), th[i][:, c0:c1], gw[i][:, c0:c1], ALU.mult)
 
         def gather(i):
             nc.vector.tensor_copy(slot(i), pages[i][:].indirect(lst3[:]))
@@ -244,21 +256,21 @@ def tile_list_rink_patch_planner_kernel(
 
         def regroup(i):
             g, t = divmod(i, PACK)
-            if t == 0:
-                joined[g] = keep.tile([P, PACK * T2], F32, name="joined", tag="big", align_bytes=64)
+            if i == 0:
+                joined[0] = keep.tile([P, PACK * T2], F32, name="joined", tag="big", align_bytes=64)[:]
+                joined[1] = joined[0]
+                joined[2] = joined[0].bitcast(BF16)[:, 0:PACK * T2]
             nc.sync.dma_start(out=joined[g][:, t * T2:(t + 1) * T2], in_=pages[i][:])
 
         def narrow(i):
             g, t = divmod(i, PACK)
-            if t == 0:
-                joined[g] = rawp.tile([P, PACK * T2], BF16, name="raw", tag="raw", align_bytes=64)
             nc.scalar.copy(out=joined[g][:, t * T2:(t + 1) * T2], in_=pages[i][:])
 
         pbs = {}
 
         def cast_planes(g, u, copy=nc.scalar.copy, into=None):
             half = T2 // 2
-            src = joined[g][:].rearrange("p (t u c i) -> p u c t i", t=PACK, u=2, i=4)
+            src = joined[g].rearrange("p (t u c i) -> p u c t i", t=PACK, u=2, i=4)
             if into is None:
                 into = ring.tile([P, half * PACK], BF16, name="pb", tag="pb", align_bytes=64)[:]
             pbs[g, u] = into
@@ -279,59 +291,77 @@ def tile_list_rink_patch_planner_kernel(
         def store_codes(g, codes):
             nc.sync.dma_start(out=out_2[g].rearrange("p m t -> p (m t)").bitcast(I32), in_=codes[:])
 
+        def store_half(g, u, codes):
+            half = T2 // 2
+            dst = out_2[g].rearrange("p m t -> p (m t)").bitcast(I32)
+            nc.sync.dma_start(out=dst[:, u * half:(u + 1) * half], in_=codes[:, u * half:(u + 1) * half])
+
+        def store_scales(g0, g1):
+            for q in range(4):
+                nc.sync.dma_start(
+                    out=out_3[g0:g1, 4 * q:4 * q + 4, :].rearrange("g r m -> r g m").bitcast(I32),
+                    in_=pscale[32 * q:32 * q + 4, g0 * T2:g1 * T2].rearrange("p (g m) -> p g m", m=T2).bitcast(I32),
+                )
+
+        def drain(j, yo, copy):
+            copy(out=yo[:, j, :], in_=ybank[j][:])
+
+        def store_y(j0, j1, yo):
+            dst = out_0[j0 * P:j1 * P, :].rearrange("(b p) m -> p b m", p=P)
+            nc.sync.dma_start(out=dst, in_=yo[:, j0:j1, :])
+
         def part(tile, k):
             return tile[:, k * PASS:(k + 1) * PASS]
 
+        deal_wgs()
         nc.vector.tensor_copy(vs[:], tabs[:].indirect(lst1[:]))
         first_codes = keep.tile([P, KP * PASS], U32, name="first_codes", align_bytes=64)
-        prep_w1(0, 0, part(first_codes, 0))
-        prep_w1(0, 1, part(first_codes, 1))
-        for a in range(KP):
-            nc.vector.tensor_copy(vw[:, a * S:(a + 1) * S], tabw[:, a * T:(a + 1) * T].bitcast(U32).indirect(lst1[:]))
-        for g in range(G):
-            factor_first(g)
+        prep_w1(0, 0, part(first_codes, 0), nc.vector.tensor_copy)
+        prep_w1(0, 1, part(first_codes, 1), nc.vector.tensor_copy)
+        for a, c0, c1 in ((0, 0, S), (1, 0, S // 2), (1, S // 2, S)):
+            window = tabw[:, a * T:(a + 1) * T].bitcast(U32)
+            nc.vector.tensor_copy(vw[:, a * S + c0:a * S + c1], window.indirect(lst1[:, c0 // 16:c1 // 16]))
+        for i in range(TILES):
+            factor(i)
+        ybank = [yps.tile([P, PICK], F32, name="ybank", tag="y%d" % j) for j in range(N // P)]
         load_page(1)
         nc.sync.dma_start(lst3[:], offs3)
         load_w1(1, 0)
         load_w1(1, 1)
-        load_page(2)
-        load_bx()
         load_w1(2, 0)
+        load_w3_scales()
+        load_page(2)
         load_w1(2, 1)
         load_page(3)
         load_w2(0)
+        load_bx()
         load_page(4)
         load_w3()
-        features(0)
-        factor(1)
+        load_page(5)
+        features(0, 0, S // 2)
+        features(0, S // 2, S)
         features(1)
         features(2)
         features(3)
-        factor(2)
-        factor(3)
-        factor(5)
-        factor(6)
-        factor(7)
-        factor(9)
-        factor(10)
-        factor(11)
-        rewrite(0)
+        scatter(0, 0, S // 2)
+        scatter(0, S // 2, S)
+        gather(0)
         rewrite(1)
-        prep_w1(1, 0, after_scatter(1, 1)[:])
+        c1 = after_scatter(1, 2)
+        prep_w1(1, 0, part(c1, 0))
+        prep_w1(1, 1, part(c1, 1))
         rewrite(2)
-        prep_w1(1, 1, after_scatter(2, 1)[:])
-        bias(0)
-        bias(1)
-        bias(2)
         features(4)
         features(5)
         features(6)
         features(7)
         rewrite(3)
+        c3 = after_scatter(3, 2)
+        prep_w1(2, 0, part(c3, 0))
+        prep_w1(2, 1, part(c3, 1))
         rewrite(4)
         regroup(0)
         regroup(1)
-        load_page(5)
         regroup(2)
         regroup(3)
         load_w2(1)
@@ -344,28 +374,28 @@ def tile_list_rink_patch_planner_kernel(
         store_page(1)
         store_page(2)
         store_page(3)
-        c4 = after_scatter(4, 2)
-        prep_w1(2, 0, part(c4, 0))
-        prep_w1(2, 1, part(c4, 1))
+        prep_w2(0, after_scatter(4, 1)[:])
+        bias(0)
+        bias(1)
+        bias(2)
         bias(3)
         rewrite(5)
-        c5 = after_scatter(5, 3)
-        prep_w2(0, part(c5, 0))
-        q0 = prep_x(0, part(c5, 1), part(c5, 2))
+        c5 = after_scatter(5, 2)
+        q0 = prep_x(0, part(c5, 0), part(c5, 1))
         q0[0]()
         q0[1]()
         second(0)
-        bias(4)
         features(8)
         features(9)
         features(10)
         features(11)
-        bias(5)
         rewrite(6)
         rewrite(7)
         c7 = after_scatter(7, 2, I32)
         planes(0, 0, c7)
         planes(0, 1, c7)
+        bias(4)
+        bias(5)
         bias(6)
         rewrite(8)
         regroup(4)
@@ -379,20 +409,21 @@ def tile_list_rink_patch_planner_kernel(
         store_page(6)
         store_page(7)
         store_codes(0, c7)
-        prep_w2(1, after_scatter(8, 1)[:])
+        c8 = after_scatter(8, 2)
+        prep_w2(1, part(c8, 0))
+        prep_w2(2, part(c8, 1))
         bias(7)
         scatter(9)
         scatter(10)
-        prep_w2(2, after_scatter(9, 1)[:])
         scatter(11)
         c11 = after_scatter(11, 2)
         q1 = prep_x(1, part(c11, 0), part(c11, 1))
         bias(8)
-        narrow(8)
-        narrow(9)
         c10 = after_scatter(10, 2, I32)
         planes(1, 0, c10)
         planes(1, 1, c10)
+        narrow(8)
+        narrow(9)
         narrow(10)
         narrow(11)
         store_page(8)
@@ -400,6 +431,7 @@ def tile_list_rink_patch_planner_kernel(
         store_page(10)
         store_page(11)
         store_codes(1, c10)
+        store_scales(0, 2)
         gather(9)
         gather(10)
         q1[0]()
@@ -418,24 +450,20 @@ def tile_list_rink_patch_planner_kernel(
         c12 = keep.tile([P, T2], I32, name="last_planes", align_bytes=64)
         c13 = keep.tile([P, 2 * PASS], U32, name="last_codes", align_bytes=64)
         quantize_planes(2, 0, c12)
+        store_half(2, 0, c12)
         xq[2] = quantize(xb2, "xq2", part(c13, 0))
         xxq[2] = quantize(xxb2, "xxq2", part(c13, 1))
         second(2)
         cast_planes(2, 1, nc.vector.tensor_copy, xxb2)
         quantize_planes(2, 1, c12)
-        store_codes(2, c12)
-
-        for q in range(4):
-            nc.sync.dma_start(
-                out=out_3[:, 4 * q:4 * q + 4, :].rearrange("g r m -> r g m").bitcast(I32),
-                in_=pscale[32 * q:32 * q + 4, :].rearrange("p (g m) -> p g m", g=G).bitcast(I32),
-            )
         yo = rawp.tile([P, N // P, PICK], F32, name="raw", tag="raw", align_bytes=64)
-        for j in range(N // P):
-            if j < N // P - 1:
-                nc.scalar.copy(out=yo[:, j, :], in_=ybank[j][:])
-            else:
-                nc.vector.tensor_copy(out=yo[:, j, :], in_=ybank[j][:])
-            if j % 2 == 1:
-                dst = out_0[(j - 1) * P:(j + 1) * P, :].rearrange("(b p) m -> p b m", b=2)
-                nc.sync.dma_start(out=dst, in_=yo[:, j - 1:j + 1, :])
+        drain(0, yo, nc.scalar.copy)
+        store_y(0, 1, yo)
+        drain(1, yo, nc.scalar.copy)
+        store_y(1, 2, yo)
+        drain(3, yo, nc.vector.tensor_copy)
+        store_y(3, 4, yo)
+        drain(2, yo, nc.scalar.copy)
+        store_y(2, 3, yo)
+        store_half(2, 1, c12)
+        store_scales(2, 3)

@@ -20,9 +20,16 @@ ALU = mybir.AluOpType
 P = 128
 PACK = 4
 PASS = P * PACK
+QUADS = 4
+PER_COL = 16
+LINE = 4
 KP = K // PASS
 G = H // PASS
 TILES = G * PACK
+BANKS = N // P
+HALF = T2 // 2
+PAGE_BUFS = 10
+STAGE_BUFS = 6
 
 
 def tile_list_rink_patch_planner_kernel(
@@ -32,300 +39,288 @@ def tile_list_rink_patch_planner_kernel(
     nc = tc.nc
     with ExitStack() as ctx:
         keep = ctx.enter_context(tc.tile_pool(name="keep", bufs=1))
-        rawp = ctx.enter_context(tc.tile_pool(name="raw", bufs=6))
+        stage = ctx.enter_context(tc.tile_pool(name="stage", bufs=STAGE_BUFS))
         ring = ctx.enter_context(tc.tile_pool(name="ring", bufs=2))
-        hps = ctx.enter_context(tc.psum_pool(name="hps", bufs=3))
-        yps = ctx.enter_context(tc.psum_pool(name="yps", bufs=1))
+        h_psum = ctx.enter_context(tc.psum_pool(name="h_psum", bufs=PACK))
+        y_psum = ctx.enter_context(tc.psum_pool(name="y_psum", bufs=1))
 
-        lst1 = keep.tile([P, S // 16], U16, name="lst1")
-        lst2 = keep.tile([P, S // 16], U16, name="lst2")
-        lst3 = keep.tile([P, PICK // 16], U16, name="lst3")
+        idx = keep.tile([P, S // PER_COL], U16, name="idx")
+        idx2 = keep.tile([P, S // PER_COL], U16, name="idx2")
+        idx3 = keep.tile([P, PICK // PER_COL], U16, name="idx3")
         gain_t = keep.tile([P, G, PACK], F32, name="gain_t")
-        bx_t = keep.tile([P, G, PACK], F32, name="bx_t")
-        tabw = keep.tile([P, KP * T], I32, name="tabw", tag="big", align_bytes=64)
-        tabs = keep.tile([P, T], U8, name="tabs", align_bytes=64)
-        wgs_t = keep.tile([P, S], F32, name="wgs_t")
-        col_pairs = [ring.tile([P, 2 * S], F32, name="cols", tag="pb", align_bytes=64) for u in range(2)]
+        bx_t = [keep.tile([P, PACK], F32, name="bx_t%d" % g) for g in range(G)]
+        tab_w = keep.tile([P, KP * T], I32, name="tab_w", tag="big", align_bytes=64)
+        tab_s = keep.tile([P, T], U8, name="tab_s", align_bytes=64)
+        wgs_rows = keep.tile([P, S], F32, name="wgs_rows")
+        col_pairs = [ring.tile([P, 2 * S], F32, name="cols", tag="page_bf", align_bytes=64) for u in range(2)]
         wgs_cols = [col_pairs[t // 2][:, (t % 2) * S:(t % 2 + 1) * S] for t in range(PACK)]
         ident = keep.tile([P, P], F32, name="ident")
-        pages = {}
-        w3w = keep.tile([P, G, 2 * N], U8, name="w3w", align_bytes=64)
-        w3s = keep.tile([P, G, N], U8, name="w3s", align_bytes=64)
-        vw = keep.tile([P, KP * S], U32, name="vw", align_bytes=64)
-        vs = keep.tile([P, S], U8, name="vs", align_bytes=64)
+        w3_w = keep.tile([P, G, 2 * N], U8, name="w3_w", align_bytes=64)
+        w3_s = keep.tile([P, G, N], U8, name="w3_s", align_bytes=64)
+        v_w = keep.tile([P, KP * S], U32, name="v_w", align_bytes=64)
+        v_s = keep.tile([P, S], U8, name="v_s", align_bytes=64)
         picked = [keep.tile([P, PACK * PICK], F32, name="picked%d" % g, align_bytes=64) for g in range(G)]
-        pscale = keep.tile([P, G * T2], U8, name="pscale", align_bytes=64)
+        page_s = keep.tile([P, G * T2], U8, name="page_s", align_bytes=64)
 
-        def rows_of(ap, g, t):
+        pages, w1_raw, w2_raw, w1_q, w2_q, x_q, xx_q = {}, {}, {}, {}, {}, {}, {}
+        wgs_dealt, factors, feats, joined, page_bf = {}, {}, {}, {}, {}
+
+        def rows_of_tile(ap, i):
+            g, t = divmod(i, PACK)
             return ap[g * PASS:(g + 1) * PASS, :].rearrange("(p t) m -> p t m", t=PACK)[:, t, :]
 
-        raw1 = {}
-        raw2 = {}
+        def stage_tile(shape, dtype):
+            return stage.tile(shape, dtype, name="staged", tag="staged", align_bytes=64)
 
         def load_w1(g, a):
-            raw1[g, a] = rawp.tile([P, PACK, PASS], F32, name="raw", tag="raw", align_bytes=64)
+            w1_raw[g, a] = stage_tile([P, PACK, PASS], F32)
             src = w1[a * PASS:(a + 1) * PASS, g * PASS:(g + 1) * PASS]
-            nc.sync.dma_start(out=raw1[g, a][:], in_=src.rearrange("(p j) c -> p j c", j=PACK))
+            nc.sync.dma_start(out=w1_raw[g, a][:], in_=src.rearrange("(p j) c -> p j c", j=PACK))
 
         def load_w2(g):
-            raw2[g] = rawp.tile([P, PACK, N], F32, name="raw", tag="raw", align_bytes=64)
-            nc.sync.dma_start(out=raw2[g][:], in_=w2[g * PASS:(g + 1) * PASS, :].rearrange("(p j) c -> p j c", j=PACK))
+            w2_raw[g] = stage_tile([P, PACK, N], F32)
+            src = w2[g * PASS:(g + 1) * PASS, :]
+            nc.sync.dma_start(out=w2_raw[g][:], in_=src.rearrange("(p j) c -> p j c", j=PACK))
 
         def load_page(i):
-            pages[i] = keep.tile([P, T2], F32, name="page", tag="page%d" % (i % 10), align_bytes=64)
-            nc.sync.dma_start(out=pages[i][:], in_=rows_of(page0, i // PACK, i % PACK))
+            pages[i] = keep.tile([P, T2], F32, name="page", tag="page%d" % (i % PAGE_BUFS), align_bytes=64)
+            nc.sync.dma_start(out=pages[i][:], in_=rows_of_tile(page0, i))
 
-        make_identity(nc, ident[:])
+        def load_bias(g):
+            nc.sync.dma_start(out=bx_t[g][:], in_=bx[g * PASS:(g + 1) * PASS].rearrange("(p t) -> p t", t=PACK))
 
-        nc.vector.memset(tabs[:].bitcast(I32), 0)
-        nc.vector.memset(w3s[:].rearrange("p g c -> p (g c)").bitcast(I32), 0)
-
-        nc.sync.dma_start(lst1[:], offs)
-        nc.sync.dma_start(out=wgs_t[:], in_=wgs)
-        nc.sync.dma_start(out=gain_t[:], in_=gain.rearrange("(g p t) -> p g t", g=G, t=PACK))
-        for q in range(4):
-            nc.sync.dma_start(
-                out=tabs[32 * q:32 * q + 4 * KP, :].bitcast(I32),
-                in_=tab_scales[:, 4 * q:4 * q + 4, :].bitcast(I32),
-            )
-        load_w1(0, 0)
-        load_w1(0, 1)
-        for a in range(KP):
-            nc.sync.dma_start(
-                out=tabw[:, a * T:(a + 1) * T],
-                in_=tab_words[a].rearrange("p t i -> p (t i)").bitcast(I32),
-            )
-        nc.sync.dma_start(lst2[:], offs2)
-        load_page(0)
-
-        def load_w3():
-            nc.sync.dma_start(out=w3w[:].bitcast(I32), in_=w3_words.rearrange("a p c -> p a c").bitcast(I32))
+        def load_w3_words():
+            nc.sync.dma_start(out=w3_w[:].bitcast(I32), in_=w3_words.rearrange("a p c -> p a c").bitcast(I32))
 
         def load_w3_scales():
-            for q in range(4):
+            for q in range(QUADS):
                 nc.sync.dma_start(
-                    out=w3s[32 * q:32 * q + 4, :, :].bitcast(I32),
+                    out=w3_s[32 * q:32 * q + 4, :, :].bitcast(I32),
                     in_=w3_scales[:, 4 * q:4 * q + 4, :].rearrange("a r c -> r a c").bitcast(I32),
                 )
 
-        def load_bx():
-            nc.sync.dma_start(out=bx_t[:], in_=bx.rearrange("(g p t) -> p g t", g=G, t=PACK))
+        def store_page(i):
+            nc.sync.dma_start(out=rows_of_tile(out_1, i), in_=pages[i][:])
 
-        def after_scatter(i, n, dtype=U32):
-            return keep.tile([P, n * PASS], dtype, name="codes", tag="gw%d" % i, align_bytes=64)
+        def store_page_codes(g, codes, c0, c1):
+            dst = out_2[g].rearrange("p m t -> p (m t)").bitcast(I32)
+            nc.sync.dma_start(out=dst[:, c0:c1], in_=codes[:, c0:c1])
 
-        def quantize(src, name, codes):
-            scales = keep.tile([P, PASS], U8, name=name + "s", align_bytes=64)
-            nc.vector.quantize_mx(out=codes.bitcast(FP8X4), scales=scales[:], in_=src[:])
+        def store_page_scales(g0, g1):
+            for q in range(QUADS):
+                nc.sync.dma_start(
+                    out=out_3[g0:g1, 4 * q:4 * q + 4, :].rearrange("g r m -> r g m").bitcast(I32),
+                    in_=page_s[32 * q:32 * q + 4, g0 * T2:g1 * T2].rearrange("p (g m) -> p g m", m=T2).bitcast(I32),
+                )
+
+        def codes_after_scatter(i, operands, dtype=U32):
+            return keep.tile([P, operands * PASS], dtype, name="codes", tag="factor%d" % i, align_bytes=64)
+
+        def operand(codes, k):
+            return codes[:, k * PASS:(k + 1) * PASS]
+
+        def quantize(src, codes, name):
+            scales = keep.tile([P, PASS], U8, name=name, align_bytes=64)
+            nc.vector.quantize_mx(out=codes.bitcast(FP8X4), scales=scales[:], in_=src)
             return codes, scales
 
         def walk_out(dst):
-            return dst.rearrange("p (c i t) -> p c t i", i=4, t=PACK)
+            return dst.rearrange("p (c i t) -> p c t i", i=LINE, t=PACK)
 
         def walk_in(src):
-            return src.rearrange("p (t c i) -> p c t i", i=4, t=PACK)
+            return src.rearrange("p (t c i) -> p c t i", i=LINE, t=PACK)
 
-        w1q = {}
-        w2q = {}
+        def weight_bf():
+            return ring.tile([P, PACK * PASS], BF16, name="weight_bf", tag="weight_bf", bufs=3, align_bytes=64)
 
-        def prep_w1(g, a, codes, copy=nc.scalar.copy):
-            wb = ring.tile([P, PASS * PACK], BF16, name="wb", tag="wb", bufs=3, align_bytes=64)
+        def prepare_w1(g, a, codes, copy):
+            rounded = weight_bf()
             copy(
-                out=wb[:].rearrange("p (t m j) -> p m j t", t=PACK, j=PACK),
-                in_=raw1[g, a][:].rearrange("p j (m t) -> p m j t", t=PACK),
+                out=rounded[:].rearrange("p (t m j) -> p m j t", t=PACK, j=PACK),
+                in_=w1_raw[g, a][:].rearrange("p j (m t) -> p m j t", t=PACK),
             )
-            w1q[g, a] = quantize(wb, "w1q%d%d" % (g, a), codes)
+            w1_q[g, a] = quantize(rounded[:], codes, "w1_s%d%d" % (g, a))
 
-        def prep_w2(g, codes):
-            wb = ring.tile([P, N * PACK], BF16, name="wb", tag="wb", bufs=3, align_bytes=64)
-            nc.scalar.copy(out=walk_out(wb[:]), in_=walk_in(raw2[g][:].rearrange("p j c -> p (j c)")))
-            w2q[g] = quantize(wb, "w2q%d" % g, codes)
+        def prepare_w2(g, codes):
+            rounded = weight_bf()
+            nc.scalar.copy(out=walk_out(rounded[:]), in_=walk_in(w2_raw[g][:].rearrange("p j c -> p (j c)")))
+            w2_q[g] = quantize(rounded[:], codes, "w2_s%d" % g)
+
+        def deal_wgs():
+            turned = h_psum.tile([P, S], F32, name="acc", tag="acc")
+            for b in range(S // P):
+                nc.tensor.transpose(turned[:, b * P:(b + 1) * P], wgs_rows[:, b * P:(b + 1) * P], ident[:])
+            by_t = turned[:].rearrange("j (b p t) -> j t b p", b=S // P, t=PACK)
+            for t in range(PACK):
+                repeated = by_t[:, t].unsqueeze(2).to_broadcast([P, S // P, QUADS, P // QUADS])
+                nc.scalar.copy(out=wgs_cols[t].rearrange("j (b q p) -> j b q p", b=S // P, q=QUADS), in_=repeated)
+                wgs_dealt[t] = y_psum.tile([P, S], F32, name="dealt", tag="y%d" % t)
+                for b in range(S // P):
+                    cols = slice(b * P, (b + 1) * P)
+                    nc.tensor.transpose(wgs_dealt[t][:, cols], wgs_cols[t][:, cols], ident[:])
+
+        def make_factors(i):
+            g, t = divmod(i, PACK)
+            factors[i] = keep.tile([P, S], F32, name="factor", tag="factor%d" % i, align_bytes=64)
+            nc.scalar.activation(out=factors[i][:], in_=wgs_dealt[t][:], func=ACT.Copy, scale=gain_t[:, g, t:t + 1])
 
         def slot(i):
-            return picked[i // PACK][:, (i % PACK) * PICK:(i % PACK + 1) * PICK]
+            g, t = divmod(i, PACK)
+            return picked[g][:, t * PICK:(t + 1) * PICK]
 
-        gw = {}
-        th = {}
-
-        def th_place(i):
-            if i == 9:
-                return slot(11)
-            if i == 10:
-                return keep.tile([P, S], F32, name="th10", tag="first_codes", align_bytes=64)[:]
-            if i == 11:
-                return picked[2][:, PICK + PICK // 2:2 * PICK + PICK // 2]
+        def feature_place(i):
+            if i == TILES - 3:
+                return slot(TILES - 1)
+            if i == TILES - 2:
+                return keep.tile([P, S], F32, name="feat", tag="first_codes", align_bytes=64)[:]
+            if i == TILES - 1:
+                return picked[G - 1][:, PICK + PICK // 2:2 * PICK + PICK // 2]
             return slot(i)
 
         def features(i, c0=0, c1=S):
             g, t = divmod(i, PACK)
-            acc = hps.tile([P, c1 - c0], F32, name="acc", tag="acc")
+            acc = h_psum.tile([P, c1 - c0], F32, name="acc", tag="acc")
             for a in range(KP):
-                codes, scales = w1q[g, a]
+                codes, scales = w1_q[g, a]
                 nc.tensor.matmul_mx(
                     out=acc[:],
                     lhsT=codes[:, t * P:(t + 1) * P].bitcast(FP8X4),
                     lhsT_scale=scales[:, t * P:(t + 1) * P],
-                    rhs=vw[:, a * S + c0:a * S + c1].bitcast(FP8X4),
-                    rhs_scale=vs[4 * a:P, c0:c1],
+                    rhs=v_w[:, a * S + c0:a * S + c1].bitcast(FP8X4),
+                    rhs_scale=v_s[4 * a:P, c0:c1],
                     start=(a == 0),
                     stop=(a == KP - 1),
                 )
             if c0 == 0:
-                th[i] = th_place(i)
-            nc.scalar.activation(out=th[i][:, c0:c1], in_=acc[:], func=ACT.Tanh)
+                feats[i] = feature_place(i)
+            nc.scalar.activation(out=feats[i][:, c0:c1], in_=acc[:], func=ACT.Tanh)
 
-        dealt = {}
+        def scatter(i, c0=0, c1=S):
+            places = idx2[:, c0 // PER_COL:c1 // PER_COL]
+            nc.vector.tensor_tensor(pages[i][:].indirect(places), feats[i][:, c0:c1], factors[i][:, c0:c1], ALU.mult)
 
-        def deal_wgs():
-            turned = hps.tile([P, S], F32, name="acc", tag="acc")
-            for b in range(S // P):
-                nc.tensor.transpose(turned[:, b * P:(b + 1) * P], wgs_t[:, b * P:(b + 1) * P], ident[:])
-            rows = turned[:].rearrange("j (b p t) -> j t b p", b=S // P, t=PACK)
-            for t in range(PACK):
-                src = rows[:, t].unsqueeze(2).to_broadcast([P, S // P, 4, 32])
-                nc.scalar.copy(out=wgs_cols[t].rearrange("j (b q p) -> j b q p", b=S // P, q=4), in_=src)
-                dealt[t] = yps.tile([P, S], F32, name="dealt", tag="y%d" % t)
-                for b in range(S // P):
-                    nc.tensor.transpose(dealt[t][:, b * P:(b + 1) * P], wgs_cols[t][:, b * P:(b + 1) * P], ident[:])
-
-        def factor(i):
-            g, t = divmod(i, PACK)
-            gw[i] = keep.tile([P, S], F32, name="gw", tag="gw%d" % i, align_bytes=64)
-            nc.scalar.activation(out=gw[i][:], in_=dealt[t][:], func=ACT.Copy, scale=gain_t[:, g, t:t + 1])
+        def gather(i):
+            nc.vector.tensor_copy(slot(i), pages[i][:].indirect(idx3[:]))
 
         def rewrite(i):
             scatter(i)
             gather(i)
 
-        def scatter(i, c0=0, c1=S):
-            places = lst2[:, c0 // 16:c1 // 16]
-            nc.vector.tensor_tensor(pages[i][:].indirect(places), th[i][:, c0:c1], gw[i][:, c0:c1], ALU.mult)
-
-        def gather(i):
-            nc.vector.tensor_copy(slot(i), pages[i][:].indirect(lst3[:]))
-
-        def store_page(i):
-            nc.sync.dma_start(out=rows_of(out_1, i // PACK, i % PACK), in_=pages[i][:])
-
-        def bias(i):
+        def add_bias(i):
             g, t = divmod(i, PACK)
-            nc.scalar.activation(out=slot(i), in_=slot(i), func=ACT.Identity, bias=bx_t[:, g, t:t + 1])
+            nc.scalar.activation(out=slot(i), in_=slot(i), func=ACT.Identity, bias=bx_t[g][:, t:t + 1])
 
-        xq = {}
-        xxq = {}
+        def round_x(g, dst, copy):
+            copy(out=walk_out(dst), in_=walk_in(picked[g][:]))
 
-        def cast_x(g, xb, copy):
-            copy(out=walk_out(xb), in_=walk_in(picked[g][:]))
+        def round_square(g, dst):
+            nc.scalar.activation(out=walk_out(dst), in_=walk_in(picked[g][:]), func=ACT.Square)
 
-        def cast_xx(g, xxb):
-            nc.scalar.activation(out=walk_out(xxb), in_=walk_in(picked[g][:]), func=ACT.Square)
+        def round_x_and_square(g):
+            x_bf = ring.tile([P, PACK * PICK], BF16, name="x_bf", tag="x_bf", bufs=1, align_bytes=64)
+            xx_bf = ring.tile([P, PACK * PICK], BF16, name="xx_bf", tag="xx_bf", bufs=1, align_bytes=64)
+            round_x(g, x_bf[:], nc.scalar.copy)
+            round_square(g, xx_bf[:])
+            return x_bf[:], xx_bf[:]
 
-        def prep_x(g, xcodes, xxcodes):
-            xb = ring.tile([P, PICK * PACK], BF16, name="xb", tag="xb", bufs=1, align_bytes=64)
-            xxb = ring.tile([P, PICK * PACK], BF16, name="xxb", tag="xxb", bufs=1, align_bytes=64)
-            cast_x(g, xb[:], nc.scalar.copy)
-            cast_xx(g, xxb[:])
-            return (lambda: xq.update({g: quantize(xb, "xq%d" % g, xcodes)}), lambda: xxq.update({g: quantize(xxb, "xxq%d" % g, xxcodes)}))
+        def quantize_x(g, src, codes):
+            x_q[g] = quantize(src, codes, "x_s%d" % g)
 
-        def second(g):
-            xc, xs = xq[g]
-            xxc, xxs = xxq[g]
-            wc, ws = w2q[g]
-            for j in range(N // P):
+        def quantize_square(g, src, codes):
+            xx_q[g] = quantize(src, codes, "xx_s%d" % g)
+
+        def scores(g):
+            for j in range(BANKS):
                 nc.tensor.matmul_mx(
-                    out=ybank[j][:],
-                    lhsT=wc[:, j * P:(j + 1) * P].bitcast(FP8X4),
-                    lhsT_scale=ws[:, j * P:(j + 1) * P],
-                    rhs=xc.bitcast(FP8X4),
-                    rhs_scale=xs[:],
+                    out=y_banks[j][:],
+                    lhsT=w2_q[g][0][:, j * P:(j + 1) * P].bitcast(FP8X4),
+                    lhsT_scale=w2_q[g][1][:, j * P:(j + 1) * P],
+                    rhs=x_q[g][0].bitcast(FP8X4),
+                    rhs_scale=x_q[g][1][:],
                     start=(g == 0),
                     stop=False,
                 )
-            for j in range(N // P):
+            for j in range(BANKS):
                 nc.tensor.matmul_mx(
-                    out=ybank[j][:],
-                    lhsT=w3w[:, g, 2 * j * P:2 * (j + 1) * P].bitcast(FP4X4),
-                    lhsT_scale=w3s[:, g, j * P:(j + 1) * P],
-                    rhs=xxc.bitcast(FP8X4),
-                    rhs_scale=xxs[:],
+                    out=y_banks[j][:],
+                    lhsT=w3_w[:, g, 2 * j * P:2 * (j + 1) * P].bitcast(FP4X4),
+                    lhsT_scale=w3_s[:, g, j * P:(j + 1) * P],
+                    rhs=xx_q[g][0].bitcast(FP8X4),
+                    rhs_scale=xx_q[g][1][:],
                     start=False,
                     stop=(g == G - 1),
                 )
 
-        joined = {}
+        def store_scores(j, staged, copy):
+            copy(out=staged[:, j, :], in_=y_banks[j][:])
+            dst = out_0[j * P:(j + 1) * P, :].rearrange("(b p) m -> p b m", p=P)
+            nc.sync.dma_start(out=dst, in_=staged[:, j:j + 1, :])
 
-        def regroup(i):
+        def join_by_dma(i):
             g, t = divmod(i, PACK)
-            if i == 0:
-                joined[0] = keep.tile([P, PACK * T2], F32, name="joined", tag="big", align_bytes=64)[:]
-                joined[1] = joined[0]
-                joined[2] = joined[0].bitcast(BF16)[:, 0:PACK * T2]
             nc.sync.dma_start(out=joined[g][:, t * T2:(t + 1) * T2], in_=pages[i][:])
 
-        def narrow(i):
+        def join_rounded(i):
             g, t = divmod(i, PACK)
             nc.scalar.copy(out=joined[g][:, t * T2:(t + 1) * T2], in_=pages[i][:])
 
-        pbs = {}
+        def page_bf_tile():
+            return ring.tile([P, PACK * HALF], BF16, name="page_bf", tag="page_bf", align_bytes=64)[:]
 
-        def cast_planes(g, u, copy=nc.scalar.copy, into=None):
-            half = T2 // 2
-            src = joined[g].rearrange("p (t u c i) -> p u c t i", t=PACK, u=2, i=4)
-            if into is None:
-                into = ring.tile([P, half * PACK], BF16, name="pb", tag="pb", align_bytes=64)[:]
-            pbs[g, u] = into
-            copy(out=walk_out(into), in_=src[:, u])
+        def interleave_page(g, u, dst, copy):
+            src = joined[g].rearrange("p (t u c i) -> p u c t i", t=PACK, u=2, i=LINE)
+            page_bf[g, u] = dst
+            copy(out=walk_out(dst), in_=src[:, u])
 
-        def quantize_planes(g, u, codes):
-            half = T2 // 2
+        def quantize_page(g, u, codes):
             nc.vector.quantize_mx(
-                out=codes[:, u * half:(u + 1) * half].bitcast(FP8X4),
-                scales=pscale[:, g * T2 + u * half:g * T2 + (u + 1) * half],
-                in_=pbs[g, u],
+                out=codes[:, u * HALF:(u + 1) * HALF].bitcast(FP8X4),
+                scales=page_s[:, g * T2 + u * HALF:g * T2 + (u + 1) * HALF],
+                in_=page_bf[g, u],
             )
 
-        def planes(g, u, codes):
-            cast_planes(g, u)
-            quantize_planes(g, u, codes)
+        def page_planes(g, codes):
+            for u in range(2):
+                interleave_page(g, u, page_bf_tile(), nc.scalar.copy)
+                quantize_page(g, u, codes)
 
-        def store_codes(g, codes):
-            nc.sync.dma_start(out=out_2[g].rearrange("p m t -> p (m t)").bitcast(I32), in_=codes[:])
+        make_identity(nc, ident[:])
+        nc.vector.memset(tab_s[:].bitcast(I32), 0)
+        nc.vector.memset(w3_s[:].rearrange("p g c -> p (g c)").bitcast(I32), 0)
 
-        def store_half(g, u, codes):
-            half = T2 // 2
-            dst = out_2[g].rearrange("p m t -> p (m t)").bitcast(I32)
-            nc.sync.dma_start(out=dst[:, u * half:(u + 1) * half], in_=codes[:, u * half:(u + 1) * half])
-
-        def store_scales(g0, g1):
-            for q in range(4):
-                nc.sync.dma_start(
-                    out=out_3[g0:g1, 4 * q:4 * q + 4, :].rearrange("g r m -> r g m").bitcast(I32),
-                    in_=pscale[32 * q:32 * q + 4, g0 * T2:g1 * T2].rearrange("p (g m) -> p g m", m=T2).bitcast(I32),
-                )
-
-        def drain(j, yo, copy):
-            copy(out=yo[:, j, :], in_=ybank[j][:])
-
-        def store_y(j0, j1, yo):
-            dst = out_0[j0 * P:j1 * P, :].rearrange("(b p) m -> p b m", p=P)
-            nc.sync.dma_start(out=dst, in_=yo[:, j0:j1, :])
-
-        def part(tile, k):
-            return tile[:, k * PASS:(k + 1) * PASS]
+        nc.sync.dma_start(idx[:], offs)
+        nc.sync.dma_start(out=wgs_rows[:], in_=wgs)
+        nc.sync.dma_start(out=gain_t[:], in_=gain.rearrange("(g p t) -> p g t", g=G, t=PACK))
+        for q in range(QUADS):
+            nc.sync.dma_start(
+                out=tab_s[32 * q:32 * q + 4 * KP, :].bitcast(I32),
+                in_=tab_scales[:, 4 * q:4 * q + 4, :].bitcast(I32),
+            )
+        for a in range(KP):
+            load_w1(0, a)
+        for a in range(KP):
+            nc.sync.dma_start(
+                out=tab_w[:, a * T:(a + 1) * T],
+                in_=tab_words[a].rearrange("p t i -> p (t i)").bitcast(I32),
+            )
+        nc.sync.dma_start(idx2[:], offs2)
+        load_page(0)
 
         deal_wgs()
-        nc.vector.tensor_copy(vs[:], tabs[:].indirect(lst1[:]))
+        nc.vector.tensor_copy(v_s[:], tab_s[:].indirect(idx[:]))
         first_codes = keep.tile([P, KP * PASS], U32, name="first_codes", align_bytes=64)
-        prep_w1(0, 0, part(first_codes, 0), nc.vector.tensor_copy)
-        prep_w1(0, 1, part(first_codes, 1), nc.vector.tensor_copy)
-        for a, c0, c1 in ((0, 0, S), (1, 0, S // 2), (1, S // 2, S)):
-            window = tabw[:, a * T:(a + 1) * T].bitcast(U32)
-            nc.vector.tensor_copy(vw[:, a * S + c0:a * S + c1], window.indirect(lst1[:, c0 // 16:c1 // 16]))
+        for a in range(KP):
+            prepare_w1(0, a, operand(first_codes, a), nc.vector.tensor_copy)
+        halves = ((0, S // 2), (S // 2, S))
+        for a, c0, c1 in [(0, 0, S)] + [(KP - 1,) + h for h in halves]:
+            window = tab_w[:, a * T:(a + 1) * T].bitcast(U32)
+            nc.vector.tensor_copy(v_w[:, a * S + c0:a * S + c1], window.indirect(idx[:, c0 // PER_COL:c1 // PER_COL]))
         for i in range(TILES):
-            factor(i)
-        ybank = [yps.tile([P, PICK], F32, name="ybank", tag="y%d" % j) for j in range(N // P)]
+            make_factors(i)
+        y_banks = [y_psum.tile([P, PICK], F32, name="y_bank", tag="y%d" % j) for j in range(BANKS)]
+
         load_page(1)
-        nc.sync.dma_start(lst3[:], offs3)
+        nc.sync.dma_start(idx3[:], offs3)
         load_w1(1, 0)
         load_w1(1, 1)
         load_w1(2, 0)
@@ -333,137 +328,117 @@ def tile_list_rink_patch_planner_kernel(
         load_page(2)
         load_w1(2, 1)
         load_page(3)
+        load_bias(0)
         load_w2(0)
-        load_bx()
         load_page(4)
-        load_w3()
+        load_w3_words()
         load_page(5)
-        features(0, 0, S // 2)
-        features(0, S // 2, S)
-        features(1)
-        features(2)
-        features(3)
-        scatter(0, 0, S // 2)
-        scatter(0, S // 2, S)
+
+        for c0, c1 in halves:
+            features(0, c0, c1)
+        for i in range(1, PACK):
+            features(i)
+        for c0, c1 in halves:
+            scatter(0, c0, c1)
         gather(0)
         rewrite(1)
-        c1 = after_scatter(1, 2)
-        prep_w1(1, 0, part(c1, 0))
-        prep_w1(1, 1, part(c1, 1))
+        codes = codes_after_scatter(1, KP)
+        for a in range(KP):
+            prepare_w1(1, a, operand(codes, a), nc.scalar.copy)
         rewrite(2)
-        features(4)
-        features(5)
-        features(6)
-        features(7)
+        for i in range(PACK, 2 * PACK):
+            features(i)
         rewrite(3)
-        c3 = after_scatter(3, 2)
-        prep_w1(2, 0, part(c3, 0))
-        prep_w1(2, 1, part(c3, 1))
+        codes = codes_after_scatter(3, KP)
+        for a in range(KP):
+            prepare_w1(2, a, operand(codes, a), nc.scalar.copy)
+
         rewrite(4)
-        regroup(0)
-        regroup(1)
-        regroup(2)
-        regroup(3)
+        joined[0] = keep.tile([P, PACK * T2], F32, name="joined", tag="big", align_bytes=64)[:]
+        joined[1] = joined[0]
+        joined[2] = joined[0].bitcast(BF16)[:, 0:PACK * T2]
+        for i in range(PACK):
+            join_by_dma(i)
+        load_bias(1)
         load_w2(1)
         load_page(6)
         load_w2(2)
-        load_page(7)
-        load_page(8)
-        load_page(9)
-        store_page(0)
-        store_page(1)
-        store_page(2)
-        store_page(3)
-        prep_w2(0, after_scatter(4, 1)[:])
-        bias(0)
-        bias(1)
-        bias(2)
-        bias(3)
+        for i in range(7, PAGE_BUFS):
+            load_page(i)
+        for i in range(PACK):
+            store_page(i)
+        for i in range(PACK):
+            add_bias(i)
+        prepare_w2(0, codes_after_scatter(4, 1)[:])
         rewrite(5)
-        c5 = after_scatter(5, 2)
-        q0 = prep_x(0, part(c5, 0), part(c5, 1))
-        q0[0]()
-        q0[1]()
-        second(0)
-        features(8)
-        features(9)
-        features(10)
-        features(11)
+        codes = codes_after_scatter(5, 2)
+        x_bf, xx_bf = round_x_and_square(0)
+        quantize_x(0, x_bf, operand(codes, 0))
+        quantize_square(0, xx_bf, operand(codes, 1))
+        scores(0)
+        for i in range(2 * PACK, TILES):
+            features(i)
         rewrite(6)
         rewrite(7)
-        c7 = after_scatter(7, 2, I32)
-        planes(0, 0, c7)
-        planes(0, 1, c7)
-        bias(4)
-        bias(5)
-        bias(6)
+        page_codes = codes_after_scatter(7, 2, I32)
+        page_planes(0, page_codes)
+        for i in range(PACK, 2 * PACK - 1):
+            add_bias(i)
+
         rewrite(8)
-        regroup(4)
-        regroup(5)
-        regroup(6)
-        regroup(7)
-        load_page(10)
-        load_page(11)
-        store_page(4)
-        store_page(5)
-        store_page(6)
-        store_page(7)
-        store_codes(0, c7)
-        c8 = after_scatter(8, 2)
-        prep_w2(1, part(c8, 0))
-        prep_w2(2, part(c8, 1))
-        bias(7)
-        scatter(9)
-        scatter(10)
-        scatter(11)
-        c11 = after_scatter(11, 2)
-        q1 = prep_x(1, part(c11, 0), part(c11, 1))
-        bias(8)
-        c10 = after_scatter(10, 2, I32)
-        planes(1, 0, c10)
-        planes(1, 1, c10)
-        narrow(8)
-        narrow(9)
-        narrow(10)
-        narrow(11)
-        store_page(8)
-        store_page(9)
-        store_page(10)
-        store_page(11)
-        store_codes(1, c10)
-        store_scales(0, 2)
+        for i in range(PACK, 2 * PACK):
+            join_by_dma(i)
+        for i in range(PAGE_BUFS, TILES):
+            load_page(i)
+        load_bias(2)
+        for i in range(PACK, 2 * PACK):
+            store_page(i)
+        store_page_codes(0, page_codes, 0, T2)
+        codes = codes_after_scatter(8, 2)
+        for g in (1, 2):
+            prepare_w2(g, operand(codes, g - 1))
+        add_bias(7)
+        for i in range(9, TILES):
+            scatter(i)
+        codes = codes_after_scatter(TILES - 1, 2)
+        x_bf, xx_bf = round_x_and_square(1)
+        add_bias(8)
+        page_codes = codes_after_scatter(TILES - 2, 2, I32)
+        page_planes(1, page_codes)
+        for i in range(2 * PACK, TILES):
+            join_rounded(i)
+        for i in range(2 * PACK, TILES):
+            store_page(i)
+        store_page_codes(1, page_codes, 0, T2)
+        store_page_scales(0, G - 1)
+
         gather(9)
         gather(10)
-        q1[0]()
+        quantize_x(1, x_bf, operand(codes, 0))
         gather(11)
-        q1[1]()
-        second(1)
-        cast_planes(2, 0)
-        bias(9)
-        bias(10)
-        bias(11)
-        last = rawp.tile([P, 2 * PICK * PACK], BF16, name="raw", tag="raw", align_bytes=64)
-        xb2 = last[:, 0:PICK * PACK]
-        xxb2 = last[:, PICK * PACK:2 * PICK * PACK]
-        cast_xx(2, xxb2)
-        cast_x(2, xb2, nc.vector.tensor_copy)
-        c12 = keep.tile([P, T2], I32, name="last_planes", align_bytes=64)
-        c13 = keep.tile([P, 2 * PASS], U32, name="last_codes", align_bytes=64)
-        quantize_planes(2, 0, c12)
-        store_half(2, 0, c12)
-        xq[2] = quantize(xb2, "xq2", part(c13, 0))
-        xxq[2] = quantize(xxb2, "xxq2", part(c13, 1))
-        second(2)
-        cast_planes(2, 1, nc.vector.tensor_copy, xxb2)
-        quantize_planes(2, 1, c12)
-        yo = rawp.tile([P, N // P, PICK], F32, name="raw", tag="raw", align_bytes=64)
-        drain(0, yo, nc.scalar.copy)
-        store_y(0, 1, yo)
-        drain(1, yo, nc.scalar.copy)
-        store_y(1, 2, yo)
-        drain(3, yo, nc.vector.tensor_copy)
-        store_y(3, 4, yo)
-        drain(2, yo, nc.scalar.copy)
-        store_y(2, 3, yo)
-        store_half(2, 1, c12)
-        store_scales(2, 3)
+        quantize_square(1, xx_bf, operand(codes, 1))
+        scores(1)
+        interleave_page(2, 0, page_bf_tile(), nc.scalar.copy)
+        for i in range(9, TILES):
+            add_bias(i)
+        both = stage_tile([P, 2 * PACK * PICK], BF16)
+        x_bf = both[:, 0:PACK * PICK]
+        xx_bf = both[:, PACK * PICK:2 * PACK * PICK]
+        round_square(2, xx_bf)
+        round_x(2, x_bf, nc.vector.tensor_copy)
+        page_codes = keep.tile([P, T2], I32, name="last_page_codes", align_bytes=64)
+        codes = keep.tile([P, 2 * PASS], U32, name="last_codes", align_bytes=64)
+        quantize_page(2, 0, page_codes)
+        store_page_codes(2, page_codes, 0, HALF)
+        quantize_x(2, x_bf, operand(codes, 0))
+        quantize_square(2, xx_bf, operand(codes, 1))
+        scores(2)
+        interleave_page(2, 1, xx_bf, nc.vector.tensor_copy)
+        quantize_page(2, 1, page_codes)
+        staged = stage_tile([P, BANKS, PICK], F32)
+        store_scores(0, staged, nc.scalar.copy)
+        store_scores(1, staged, nc.scalar.copy)
+        store_scores(3, staged, nc.vector.tensor_copy)
+        store_scores(2, staged, nc.scalar.copy)
+        store_page_codes(2, page_codes, HALF, T2)
+        store_page_scales(G - 1, G)

@@ -29,6 +29,7 @@ TILES = G * PACK
 BANKS = N // P
 HALF = T2 // 2
 PAGE_BUFS = 10
+LAST_COLS = 64
 STAGE_BUFS = 6
 
 
@@ -62,7 +63,7 @@ def tile_list_rink_patch_planner_kernel(
         picked = [keep.tile([P, PACK * PICK], F32, name="picked%d" % g, align_bytes=64) for g in range(G)]
         page_s = keep.tile([P, G * T2], U8, name="page_s", align_bytes=64)
 
-        pages, w1_raw, w2_raw, w1_q, w2_q, x_q, xx_q = {}, {}, {}, {}, {}, {}, {}
+        pages, w1_raw, w2_raw, w2_bf, w1_q, w2_q, x_q, xx_q = {}, {}, {}, {}, {}, {}, {}, {}
         wgs_dealt, factors, feats, joined, page_bf = {}, {}, {}, {}, {}
 
         def rows_of_tile(ap, i):
@@ -82,9 +83,22 @@ def tile_list_rink_patch_planner_kernel(
             src = w2[g * PASS:(g + 1) * PASS, :]
             nc.sync.dma_start(out=w2_raw[g][:], in_=src.rearrange("(p j) c -> p j c", j=PACK))
 
+        def page_tile(i):
+            return keep.tile([P, T2], F32, name="page", tag="page%d" % (i % PAGE_BUFS), align_bytes=64)
+
         def load_page(i):
-            pages[i] = keep.tile([P, T2], F32, name="page", tag="page%d" % (i % PAGE_BUFS), align_bytes=64)
+            pages[i] = page_tile(i)
             nc.sync.dma_start(out=pages[i][:], in_=rows_of_tile(page0, i))
+
+        def begin_page_pair(i):
+            pages[i + 1] = page_tile(i + 1)
+            cols = slice(0, T2 - LAST_COLS)
+            nc.sync.dma_start(out=pages[i + 1][:, cols], in_=rows_of_tile(page0, i + 1)[:, cols])
+
+        def end_page_pair(i):
+            load_page(i)
+            cols = slice(T2 - LAST_COLS, T2)
+            nc.sync.dma_start(out=pages[i + 1][:, cols], in_=rows_of_tile(page0, i + 1)[:, cols])
 
         def load_bias(g):
             nc.sync.dma_start(out=bx_t[g][:], in_=bx[g * PASS:(g + 1) * PASS].rearrange("(p t) -> p t", t=PACK))
@@ -102,9 +116,8 @@ def tile_list_rink_patch_planner_kernel(
         def store_page(i):
             nc.sync.dma_start(out=rows_of_tile(out_1, i), in_=pages[i][:])
 
-        def store_page_codes(g, codes, c0, c1):
-            dst = out_2[g].rearrange("p m t -> p (m t)").bitcast(I32)
-            nc.sync.dma_start(out=dst[:, c0:c1], in_=codes[:, c0:c1])
+        def store_page_codes(g, codes):
+            nc.sync.dma_start(out=out_2[g].rearrange("p m t -> p (m t)").bitcast(I32), in_=codes[:])
 
         def store_page_scales(g0, g1):
             for q in range(QUADS):
@@ -141,10 +154,12 @@ def tile_list_rink_patch_planner_kernel(
             )
             w1_q[g, a] = quantize(rounded[:], codes, "w1_s%d%d" % (g, a))
 
-        def prepare_w2(g, codes):
-            rounded = weight_bf()
-            nc.scalar.copy(out=walk_out(rounded[:]), in_=walk_in(w2_raw[g][:].rearrange("p j c -> p (j c)")))
-            w2_q[g] = quantize(rounded[:], codes, "w2_s%d" % g)
+        def round_w2(g):
+            w2_bf[g] = weight_bf()
+            nc.scalar.copy(out=walk_out(w2_bf[g][:]), in_=walk_in(w2_raw[g][:].rearrange("p j c -> p (j c)")))
+
+        def quantize_w2(g, codes):
+            w2_q[g] = quantize(w2_bf[g][:], codes, "w2_s%d" % g)
 
         def deal_wgs():
             turned = h_psum.tile([P, S], F32, name="acc", tag="acc")
@@ -169,11 +184,13 @@ def tile_list_rink_patch_planner_kernel(
             return picked[g][:, t * PICK:(t + 1) * PICK]
 
         def feature_place(i):
-            if i == TILES - 3:
-                return slot(TILES - 1)
-            if i == TILES - 2:
+            if i == 8:
                 return keep.tile([P, S], F32, name="feat", tag="first_codes", align_bytes=64)[:]
-            if i == TILES - 1:
+            if i == 9:
+                return slot(11)
+            if i == 10:
+                return slot(8)
+            if i == 11:
                 return picked[G - 1][:, PICK + PICK // 2:2 * PICK + PICK // 2]
             return slot(i)
 
@@ -205,6 +222,12 @@ def tile_list_rink_patch_planner_kernel(
         def rewrite(i):
             scatter(i)
             gather(i)
+
+        def rewrite_pair(i):
+            scatter(i)
+            scatter(i + 1)
+            gather(i)
+            gather(i + 1)
 
         def add_bias(i):
             g, t = divmod(i, PACK)
@@ -253,8 +276,7 @@ def tile_list_rink_patch_planner_kernel(
 
         def store_scores(j, staged, copy):
             copy(out=staged[:, j, :], in_=y_banks[j][:])
-            dst = out_0[j * P:(j + 1) * P, :].rearrange("(b p) m -> p b m", p=P)
-            nc.sync.dma_start(out=dst, in_=staged[:, j:j + 1, :])
+            nc.sync.dma_start(out=out_0[j * P:(j + 1) * P, :], in_=staged[:, j, :])
 
         def join_by_dma(i):
             g, t = divmod(i, PACK)
@@ -264,13 +286,10 @@ def tile_list_rink_patch_planner_kernel(
             g, t = divmod(i, PACK)
             nc.scalar.copy(out=joined[g][:, t * T2:(t + 1) * T2], in_=pages[i][:])
 
-        def page_bf_tile():
-            return ring.tile([P, PACK * HALF], BF16, name="page_bf", tag="page_bf", align_bytes=64)[:]
-
-        def interleave_page(g, u, dst, copy):
+        def interleave_page(g, u):
             src = joined[g].rearrange("p (t u c i) -> p u c t i", t=PACK, u=2, i=LINE)
-            page_bf[g, u] = dst
-            copy(out=walk_out(dst), in_=src[:, u])
+            page_bf[g, u] = ring.tile([P, PACK * HALF], BF16, name="page_bf", tag="page_bf", align_bytes=64)[:]
+            nc.scalar.copy(out=walk_out(page_bf[g, u]), in_=src[:, u])
 
         def quantize_page(g, u, codes):
             nc.vector.quantize_mx(
@@ -281,7 +300,7 @@ def tile_list_rink_patch_planner_kernel(
 
         def page_planes(g, codes):
             for u in range(2):
-                interleave_page(g, u, page_bf_tile(), nc.scalar.copy)
+                interleave_page(g, u)
                 quantize_page(g, u, codes)
 
         make_identity(nc, ident[:])
@@ -330,9 +349,10 @@ def tile_list_rink_patch_planner_kernel(
         load_page(3)
         load_bias(0)
         load_w2(0)
-        load_page(4)
+        begin_page_pair(4)
+        load_w2(1)
+        end_page_pair(4)
         load_w3_words()
-        load_page(5)
 
         for c0, c1 in halves:
             features(0, c0, c1)
@@ -353,24 +373,24 @@ def tile_list_rink_patch_planner_kernel(
         for a in range(KP):
             prepare_w1(2, a, operand(codes, a), nc.scalar.copy)
 
-        rewrite(4)
+        rewrite_pair(4)
         joined[0] = keep.tile([P, PACK * T2], F32, name="joined", tag="big", align_bytes=64)[:]
         joined[1] = joined[0]
         joined[2] = joined[0].bitcast(BF16)[:, 0:PACK * T2]
         for i in range(PACK):
             join_by_dma(i)
         load_bias(1)
-        load_w2(1)
-        load_page(6)
+        begin_page_pair(6)
         load_w2(2)
-        for i in range(7, PAGE_BUFS):
+        end_page_pair(6)
+        for i in range(2 * PACK, PAGE_BUFS):
             load_page(i)
         for i in range(PACK):
             store_page(i)
         for i in range(PACK):
             add_bias(i)
-        prepare_w2(0, codes_after_scatter(4, 1)[:])
-        rewrite(5)
+        round_w2(0)
+        quantize_w2(0, codes_after_scatter(4, 1)[:])
         codes = codes_after_scatter(5, 2)
         x_bf, xx_bf = round_x_and_square(0)
         quantize_x(0, x_bf, operand(codes, 0))
@@ -378,67 +398,65 @@ def tile_list_rink_patch_planner_kernel(
         scores(0)
         for i in range(2 * PACK, TILES):
             features(i)
-        rewrite(6)
-        rewrite(7)
+        rewrite_pair(6)
         page_codes = codes_after_scatter(7, 2, I32)
         page_planes(0, page_codes)
         for i in range(PACK, 2 * PACK - 1):
             add_bias(i)
 
-        rewrite(8)
+        scatter(8)
+        scatter(9)
         for i in range(PACK, 2 * PACK):
             join_by_dma(i)
-        for i in range(PAGE_BUFS, TILES):
-            load_page(i)
+        begin_page_pair(10)
+        end_page_pair(10)
         load_bias(2)
         for i in range(PACK, 2 * PACK):
             store_page(i)
-        store_page_codes(0, page_codes, 0, T2)
-        codes = codes_after_scatter(8, 2)
+        store_page_codes(0, page_codes)
+        scatter(10)
+        scatter(11)
+        codes = codes_after_scatter(TILES - 1, 4)
         for g in (1, 2):
-            prepare_w2(g, operand(codes, g - 1))
+            round_w2(g)
         add_bias(7)
-        for i in range(9, TILES):
-            scatter(i)
-        codes = codes_after_scatter(TILES - 1, 2)
         x_bf, xx_bf = round_x_and_square(1)
-        add_bias(8)
         page_codes = codes_after_scatter(TILES - 2, 2, I32)
-        page_planes(1, page_codes)
+        for u in range(2):
+            interleave_page(1, u)
         for i in range(2 * PACK, TILES):
             join_rounded(i)
         for i in range(2 * PACK, TILES):
             store_page(i)
-        store_page_codes(1, page_codes, 0, T2)
-        store_page_scales(0, G - 1)
 
+        gather(8)
+        for u in range(2):
+            quantize_page(1, u, page_codes)
+        store_page_codes(1, page_codes)
+        store_page_scales(0, G - 1)
         gather(9)
+        for g in (1, 2):
+            quantize_w2(g, operand(codes, g - 1))
         gather(10)
-        quantize_x(1, x_bf, operand(codes, 0))
+        quantize_x(1, x_bf, operand(codes, 2))
         gather(11)
-        quantize_square(1, xx_bf, operand(codes, 1))
+        quantize_square(1, xx_bf, operand(codes, 3))
         scores(1)
-        interleave_page(2, 0, page_bf_tile(), nc.scalar.copy)
-        for i in range(9, TILES):
+        page_codes = keep.tile([P, T2], I32, name="last_page_codes", align_bytes=64)
+        page_planes(2, page_codes)
+        store_page_codes(2, page_codes)
+        store_page_scales(G - 1, G)
+        for i in range(2 * PACK, TILES):
             add_bias(i)
         both = stage_tile([P, 2 * PACK * PICK], BF16)
         x_bf = both[:, 0:PACK * PICK]
         xx_bf = both[:, PACK * PICK:2 * PACK * PICK]
         round_square(2, xx_bf)
         round_x(2, x_bf, nc.vector.tensor_copy)
-        page_codes = keep.tile([P, T2], I32, name="last_page_codes", align_bytes=64)
         codes = keep.tile([P, 2 * PASS], U32, name="last_codes", align_bytes=64)
-        quantize_page(2, 0, page_codes)
-        store_page_codes(2, page_codes, 0, HALF)
         quantize_x(2, x_bf, operand(codes, 0))
         quantize_square(2, xx_bf, operand(codes, 1))
         scores(2)
-        interleave_page(2, 1, xx_bf, nc.vector.tensor_copy)
-        quantize_page(2, 1, page_codes)
         staged = stage_tile([P, BANKS, PICK], F32)
-        store_scores(0, staged, nc.scalar.copy)
-        store_scores(1, staged, nc.scalar.copy)
-        store_scores(3, staged, nc.vector.tensor_copy)
-        store_scores(2, staged, nc.scalar.copy)
-        store_page_codes(2, page_codes, HALF, T2)
-        store_page_scales(G - 1, G)
+        for j in range(BANKS):
+            store_scores(j, staged, nc.vector.tensor_copy if j % 2 else nc.scalar.copy)

@@ -103,10 +103,8 @@ def tile_list_rink_patch_planner_kernel(
         def load_bias(g):
             nc.sync.dma_start(out=bx_t[g][:], in_=bx[g * PASS:(g + 1) * PASS].rearrange("(p t) -> p t", t=PACK))
 
-        def load_w3_words():
+        def load_w3():
             nc.sync.dma_start(out=w3_w[:].bitcast(I32), in_=w3_words.rearrange("a p c -> p a c").bitcast(I32))
-
-        def load_w3_scales():
             for q in range(QUADS):
                 nc.sync.dma_start(
                     out=w3_s[32 * q:32 * q + 4, :, :].bitcast(I32),
@@ -343,16 +341,15 @@ def tile_list_rink_patch_planner_kernel(
         load_w1(1, 0)
         load_w1(1, 1)
         load_w1(2, 0)
-        load_w3_scales()
-        load_page(2)
+        begin_page_pair(2)
+        end_page_pair(2)
         load_w1(2, 1)
-        load_page(3)
         load_bias(0)
         load_w2(0)
         begin_page_pair(4)
         load_w2(1)
         end_page_pair(4)
-        load_w3_words()
+        load_w3()
 
         for c0, c1 in halves:
             features(0, c0, c1)
@@ -365,10 +362,9 @@ def tile_list_rink_patch_planner_kernel(
         codes = codes_after_scatter(1, KP)
         for a in range(KP):
             prepare_w1(1, a, operand(codes, a), nc.scalar.copy)
-        rewrite(2)
+        rewrite_pair(2)
         for i in range(PACK, 2 * PACK):
             features(i)
-        rewrite(3)
         codes = codes_after_scatter(3, KP)
         for a in range(KP):
             prepare_w1(2, a, operand(codes, a), nc.scalar.copy)
@@ -438,8 +434,8 @@ def tile_list_rink_patch_planner_kernel(
         for g in (1, 2):
             quantize_w2(g, operand(codes, g - 1))
         gather(10)
-        quantize_x(1, x_bf, operand(codes, 2))
         gather(11)
+        quantize_x(1, x_bf, operand(codes, 2))
         quantize_square(1, xx_bf, operand(codes, 3))
         scores(1)
         page_codes = keep.tile([P, T2], I32, name="last_page_codes", align_bytes=64)

from contextlib import ExitStack

import concourse.mybir as mybir
from concourse.masks import make_identity

K, H, N, T, S, T2, PICK = 1024, 1536, 512, 2048, 512, 1024, 512
FLOPS = 2 * K * H * S + 2 * 2 * H * N * PICK

F32 = mybir.dt.float32
BF16 = mybir.dt.bfloat16
I32 = mybir.dt.int32
U32 = mybir.dt.uint32
U16 = mybir.dt.uint16
U8 = mybir.dt.uint8
FP8X4 = mybir.dt.float8_e4m3fn_x4
FP4X4 = mybir.dt.float4_e2m1fn_x4
ACT = mybir.ActivationFunctionType
ALU = mybir.AluOpType

P = 128
PACK = 4
PASS = P * PACK
QUADS = 4
PER_COL = 16
LINE = 4
KP = K // PASS
G = H // PASS
TILES = G * PACK
BANKS = N // P
HALF = T2 // 2
PAGE_BUFS = 10
LAST_COLS = 64
STAGE_BUFS = 6


def tile_list_rink_patch_planner_kernel(
    tc, tab_words, tab_scales, offs, offs2, offs3, w1, gain, wgs, page0, bx, w2, w3_words, w3_scales,
    out_0, out_1, out_2, out_3,
):
    nc = tc.nc
    with ExitStack() as ctx:
        keep = ctx.enter_context(tc.tile_pool(name="keep", bufs=1))
        stage = ctx.enter_context(tc.tile_pool(name="stage", bufs=STAGE_BUFS))
        ring = ctx.enter_context(tc.tile_pool(name="ring", bufs=2))
        h_psum = ctx.enter_context(tc.psum_pool(name="h_psum", bufs=PACK))
        y_psum = ctx.enter_context(tc.psum_pool(name="y_psum", bufs=1))

        idx = keep.tile([P, S // PER_COL], U16, name="idx")
        idx2 = keep.tile([P, S // PER_COL], U16, name="idx2")
        idx3 = keep.tile([P, PICK // PER_COL], U16, name="idx3")
        gain_t = keep.tile([P, G, PACK], F32, name="gain_t")
        bx_t = [keep.tile([P, PACK], F32, name="bx_t%d" % g) for g in range(G)]
        tab_w = keep.tile([P, KP * T], I32, name="tab_w", tag="big", align_bytes=64)
        tab_s = keep.tile([P, T], U8, name="tab_s", align_bytes=64)
        wgs_rows = keep.tile([P, S], F32, name="wgs_rows")
        col_pairs = [ring.tile([P, 2 * S], F32, name="cols", tag="page_bf", align_bytes=64) for u in range(2)]
        wgs_cols = [col_pairs[t // 2][:, (t % 2) * S:(t % 2 + 1) * S] for t in range(PACK)]
        ident = keep.tile([P, P], F32, name="ident")
        w3_w = keep.tile([P, G, 2 * N], U8, name="w3_w", align_bytes=64)
        w3_s = keep.tile([P, G, N], U8, name="w3_s", align_bytes=64)
        v_w = keep.tile([P, KP * S], U32, name="v_w", align_bytes=64)
        v_s = keep.tile([P, S], U8, name="v_s", align_bytes=64)
        picked = [keep.tile([P, PACK * PICK], F32, name="picked%d" % g, align_bytes=64) for g in range(G)]
        page_s = keep.tile([P, G * T2], U8, name="page_s", align_bytes=64)

        pages, w1_raw, w2_raw, w2_bf, w1_q, w2_q, x_q, xx_q = {}, {}, {}, {}, {}, {}, {}, {}
        wgs_dealt, factors, feats, joined, page_bf = {}, {}, {}, {}, {}

        def rows_of_tile(ap, i):
            g, t = divmod(i, PACK)
            return ap[g * PASS:(g + 1) * PASS, :].rearrange("(p t) m -> p t m", t=PACK)[:, t, :]

        def stage_tile(shape, dtype):
            return stage.tile(shape, dtype, name="staged", tag="staged", align_bytes=64)

        def load_w1(g, a):
            w1_raw[g, a] = stage_tile([P, PACK, PASS], F32)
            src = w1[a * PASS:(a + 1) * PASS, g * PASS:(g + 1) * PASS]
            nc.sync.dma_start(out=w1_raw[g, a][:], in_=src.rearrange("(p j) c -> p j c", j=PACK))

        def load_w2(g):
            w2_raw[g] = stage_tile([P, PACK, N], F32)
            src = w2[g * PASS:(g + 1) * PASS, :]
            nc.sync.dma_start(out=w2_raw[g][:], in_=src.rearrange("(p j) c -> p j c", j=PACK))

        def page_tile(i):
            return keep.tile([P, T2], F32, name="page", tag="page%d" % (i % PAGE_BUFS), align_bytes=64)

        def load_page(i):
            pages[i] = page_tile(i)
            nc.sync.dma_start(out=pages[i][:], in_=rows_of_tile(page0, i))

        def begin_page_pair(i):
            pages[i + 1] = page_tile(i + 1)
            cols = slice(0, T2 - LAST_COLS)
            nc.sync.dma_start(out=pages[i + 1][:, cols], in_=rows_of_tile(page0, i + 1)[:, cols])

        def end_page_pair(i):
            load_page(i)
            cols = slice(T2 - LAST_COLS, T2)
            nc.sync.dma_start(out=pages[i + 1][:, cols], in_=rows_of_tile(page0, i + 1)[:, cols])

        def load_bias(g):
            nc.sync.dma_start(out=bx_t[g][:], in_=bx[g * PASS:(g + 1) * PASS].rearrange("(p t) -> p t", t=PACK))

        def load_w3():
            nc.sync.dma_start(out=w3_w[:].bitcast(I32), in_=w3_words.rearrange("a p c -> p a c").bitcast(I32))
            for q in range(QUADS):
                nc.sync.dma_start(
                    out=w3_s[32 * q:32 * q + 4, :, :].bitcast(I32),
                    in_=w3_scales[:, 4 * q:4 * q + 4, :].rearrange("a r c -> r a c").bitcast(I32),
                )

        def store_page(i):
            nc.sync.dma_start(out=rows_of_tile(out_1, i), in_=pages[i][:])

        def store_page_codes(g, codes):
            nc.sync.dma_start(out=out_2[g].rearrange("p m t -> p (m t)").bitcast(I32), in_=codes[:])

        def store_page_scales(g0, g1):
            for q in range(QUADS):
                nc.sync.dma_start(
                    out=out_3[g0:g1, 4 * q:4 * q + 4, :].rearrange("g r m -> r g m").bitcast(I32),
                    in_=page_s[32 * q:32 * q + 4, g0 * T2:g1 * T2].rearrange("p (g m) -> p g m", m=T2).bitcast(I32),
                )

        def codes_after_scatter(i, operands, dtype=U32):
            return keep.tile([P, operands * PASS], dtype, name="codes", tag="factor%d" % i, align_bytes=64)

        def operand(codes, k):
            return codes[:, k * PASS:(k + 1) * PASS]

        def quantize(src, codes, name):
            scales = keep.tile([P, PASS], U8, name=name, align_bytes=64)
            nc.vector.quantize_mx(out=codes.bitcast(FP8X4), scales=scales[:], in_=src)
            return codes, scales

        def walk_out(dst):
            return dst.rearrange("p (c i t) -> p c t i", i=LINE, t=PACK)

        def walk_in(src):
            return src.rearrange("p (t c i) -> p c t i", i=LINE, t=PACK)

        def weight_bf():
            return ring.tile([P, PACK * PASS], BF16, name="weight_bf", tag="weight_bf", bufs=3, align_bytes=64)

        def prepare_w1(g, a, codes, copy):
            rounded = weight_bf()
            copy(
                out=rounded[:].rearrange("p (t m j) -> p m j t", t=PACK, j=PACK),
                in_=w1_raw[g, a][:].rearrange("p j (m t) -> p m j t", t=PACK),
            )
            w1_q[g, a] = quantize(rounded[:], codes, "w1_s%d%d" % (g, a))

        def round_w2(g):
            w2_bf[g] = weight_bf()
            nc.scalar.copy(out=walk_out(w2_bf[g][:]), in_=walk_in(w2_raw[g][:].rearrange("p j c -> p (j c)")))

        def quantize_w2(g, codes):
            w2_q[g] = quantize(w2_bf[g][:], codes, "w2_s%d" % g)

        def deal_wgs():
            turned = h_psum.tile([P, S], F32, name="acc", tag="acc")
            for b in range(S // P):
                nc.tensor.transpose(turned[:, b * P:(b + 1) * P], wgs_rows[:, b * P:(b + 1) * P], ident[:])
            by_t = turned[:].rearrange("j (b p t) -> j t b p", b=S // P, t=PACK)
            for t in range(PACK):
                repeated = by_t[:, t].unsqueeze(2).to_broadcast([P, S // P, QUADS, P // QUADS])
                nc.scalar.copy(out=wgs_cols[t].rearrange("j (b q p) -> j b q p", b=S // P, q=QUADS), in_=repeated)
                wgs_dealt[t] = y_psum.tile([P, S], F32, name="dealt", tag="y%d" % t)
                for b in range(S // P):
                    cols = slice(b * P, (b + 1) * P)
                    nc.tensor.transpose(wgs_dealt[t][:, cols], wgs_cols[t][:, cols], ident[:])

        def make_factors(i):
            g, t = divmod(i, PACK)
            factors[i] = keep.tile([P, S], F32, name="factor", tag="factor%d" % i, align_bytes=64)
            nc.scalar.activation(out=factors[i][:], in_=wgs_dealt[t][:], func=ACT.Copy, scale=gain_t[:, g, t:t + 1])

        def slot(i):
            g, t = divmod(i, PACK)
            return picked[g][:, t * PICK:(t + 1) * PICK]

        def feature_place(i):
            if i == 8:
                return keep.tile([P, S], F32, name="feat", tag="first_codes", align_bytes=64)[:]
            if i == 9:
                return slot(11)
            if i == 10:
                return slot(8)
            if i == 11:
                return picked[G - 1][:, PICK + PICK // 2:2 * PICK + PICK // 2]
            return slot(i)

        def features(i, c0=0, c1=S):
            g, t = divmod(i, PACK)
            acc = h_psum.tile([P, c1 - c0], F32, name="acc", tag="acc")
            for a in range(KP):
                codes, scales = w1_q[g, a]
                nc.tensor.matmul_mx(
                    out=acc[:],
                    lhsT=codes[:, t * P:(t + 1) * P].bitcast(FP8X4),
                    lhsT_scale=scales[:, t * P:(t + 1) * P],
                    rhs=v_w[:, a * S + c0:a * S + c1].bitcast(FP8X4),
                    rhs_scale=v_s[4 * a:P, c0:c1],
                    start=(a == 0),
                    stop=(a == KP - 1),
                )
            if c0 == 0:
                feats[i] = feature_place(i)
            nc.scalar.activation(out=feats[i][:, c0:c1], in_=acc[:], func=ACT.Tanh)

        def scatter(i, c0=0, c1=S):
            places = idx2[:, c0 // PER_COL:c1 // PER_COL]
            nc.vector.tensor_tensor(pages[i][:].indirect(places), feats[i][:, c0:c1], factors[i][:, c0:c1], ALU.mult)

        def gather(i):
            nc.vector.tensor_copy(slot(i), pages[i][:].indirect(idx3[:]))

        def rewrite(i):
            scatter(i)
            gather(i)

        def rewrite_pair(i):
            scatter(i)
            scatter(i + 1)
            gather(i)
            gather(i + 1)

        def add_bias(i):
            g, t = divmod(i, PACK)
            nc.scalar.activation(out=slot(i), in_=slot(i), func=ACT.Identity, bias=bx_t[g][:, t:t + 1])

        def round_x(g, dst, copy):
            copy(out=walk_out(dst), in_=walk_in(picked[g][:]))

        def round_square(g, dst):
            nc.scalar.activation(out=walk_out(dst), in_=walk_in(picked[g][:]), func=ACT.Square)

        def round_x_and_square(g):
            x_bf = ring.tile([P, PACK * PICK], BF16, name="x_bf", tag="x_bf", bufs=1, align_bytes=64)
            xx_bf = ring.tile([P, PACK * PICK], BF16, name="xx_bf", tag="xx_bf", bufs=1, align_bytes=64)
            round_x(g, x_bf[:], nc.scalar.copy)
            round_square(g, xx_bf[:])
            return x_bf[:], xx_bf[:]

        def quantize_x(g, src, codes):
            x_q[g] = quantize(src, codes, "x_s%d" % g)

        def quantize_square(g, src, codes):
            xx_q[g] = quantize(src, codes, "xx_s%d" % g)

        def scores(g):
            for j in range(BANKS):
                nc.tensor.matmul_mx(
                    out=y_banks[j][:],
                    lhsT=w2_q[g][0][:, j * P:(j + 1) * P].bitcast(FP8X4),
                    lhsT_scale=w2_q[g][1][:, j * P:(j + 1) * P],
                    rhs=x_q[g][0].bitcast(FP8X4),
                    rhs_scale=x_q[g][1][:],
                    start=(g == 0),
                    stop=False,
                )
            for j in range(BANKS):
                nc.tensor.matmul_mx(
                    out=y_banks[j][:],
                    lhsT=w3_w[:, g, 2 * j * P:2 * (j + 1) * P].bitcast(FP4X4),
                    lhsT_scale=w3_s[:, g, j * P:(j + 1) * P],
                    rhs=xx_q[g][0].bitcast(FP8X4),
                    rhs_scale=xx_q[g][1][:],
                    start=False,
                    stop=(g == G - 1),
                )

        def store_scores(j, staged, copy):
            copy(out=staged[:, j, :], in_=y_banks[j][:])
            nc.sync.dma_start(out=out_0[j * P:(j + 1) * P, :], in_=staged[:, j, :])

        def join_by_dma(i):
            g, t = divmod(i, PACK)
            nc.sync.dma_start(out=joined[g][:, t * T2:(t + 1) * T2], in_=pages[i][:])

        def join_rounded(i):
            g, t = divmod(i, PACK)
            nc.scalar.copy(out=joined[g][:, t * T2:(t + 1) * T2], in_=pages[i][:])

        def interleave_page(g, u):
            src = joined[g].rearrange("p (t u c i) -> p u c t i", t=PACK, u=2, i=LINE)
            page_bf[g, u] = ring.tile([P, PACK * HALF], BF16, name="page_bf", tag="page_bf", align_bytes=64)[:]
            nc.scalar.copy(out=walk_out(page_bf[g, u]), in_=src[:, u])

        def quantize_page(g, u, codes):
            nc.vector.quantize_mx(
                out=codes[:, u * HALF:(u + 1) * HALF].bitcast(FP8X4),
                scales=page_s[:, g * T2 + u * HALF:g * T2 + (u + 1) * HALF],
                in_=page_bf[g, u],
            )

        def page_planes(g, codes):
            for u in range(2):
                interleave_page(g, u)
                quantize_page(g, u, codes)

        make_identity(nc, ident[:])
        nc.vector.memset(tab_s[:].bitcast(I32), 0)
        nc.vector.memset(w3_s[:].rearrange("p g c -> p (g c)").bitcast(I32), 0)

        nc.sync.dma_start(idx[:], offs)
        nc.sync.dma_start(out=wgs_rows[:], in_=wgs)
        nc.sync.dma_start(out=gain_t[:], in_=gain.rearrange("(g p t) -> p g t", g=G, t=PACK))
        for q in range(QUADS):
            nc.sync.dma_start(
                out=tab_s[32 * q:32 * q + 4 * KP, :].bitcast(I32),
                in_=tab_scales[:, 4 * q:4 * q + 4, :].bitcast(I32),
            )
        for a in range(KP):
            load_w1(0, a)
        for a in range(KP):
            nc.sync.dma_start(
                out=tab_w[:, a * T:(a + 1) * T],
                in_=tab_words[a].rearrange("p t i -> p (t i)").bitcast(I32),
            )
        nc.sync.dma_start(idx2[:], offs2)
        load_page(0)

        deal_wgs()
        nc.vector.tensor_copy(v_s[:], tab_s[:].indirect(idx[:]))
        first_codes = keep.tile([P, KP * PASS], U32, name="first_codes", align_bytes=64)
        for a in range(KP):
            prepare_w1(0, a, operand(first_codes, a), nc.vector.tensor_copy)
        halves = ((0, S // 2), (S // 2, S))
        for a, c0, c1 in [(0, 0, S)] + [(KP - 1,) + h for h in halves]:
            window = tab_w[:, a * T:(a + 1) * T].bitcast(U32)
            nc.vector.tensor_copy(v_w[:, a * S + c0:a * S + c1], window.indirect(idx[:, c0 // PER_COL:c1 // PER_COL]))
        for i in range(TILES):
            make_factors(i)
        y_banks = [y_psum.tile([P, PICK], F32, name="y_bank", tag="y%d" % j) for j in range(BANKS)]

        load_page(1)
        nc.sync.dma_start(idx3[:], offs3)
        load_w1(1, 0)
        load_w1(1, 1)
        load_w1(2, 0)
        begin_page_pair(2)
        end_page_pair(2)
        load_w1(2, 1)
        load_bias(0)
        load_w2(0)
        begin_page_pair(4)
        load_w2(1)
        end_page_pair(4)
        load_w3()

        for c0, c1 in halves:
            features(0, c0, c1)
        for i in range(1, PACK):
            features(i)
        for c0, c1 in halves:
            scatter(0, c0, c1)
        gather(0)
        rewrite(1)
        codes = codes_after_scatter(1, KP)
        for a in range(KP):
            prepare_w1(1, a, operand(codes, a), nc.scalar.copy)
        rewrite_pair(2)
        for i in range(PACK, 2 * PACK):
            features(i)
        codes = codes_after_scatter(3, KP)
        for a in range(KP):
            prepare_w1(2, a, operand(codes, a), nc.scalar.copy)

        rewrite_pair(4)
        joined[0] = keep.tile([P, PACK * T2], F32, name="joined", tag="big", align_bytes=64)[:]
        joined[1] = joined[0]
        joined[2] = joined[0].bitcast(BF16)[:, 0:PACK * T2]
        for i in range(PACK):
            join_by_dma(i)
        load_bias(1)
        begin_page_pair(6)
        load_w2(2)
        end_page_pair(6)
        for i in range(2 * PACK, PAGE_BUFS):
            load_page(i)
        for i in range(PACK):
            store_page(i)
        for i in range(PACK):
            add_bias(i)
        round_w2(0)
        quantize_w2(0, codes_after_scatter(4, 1)[:])
        codes = codes_after_scatter(5, 2)
        x_bf, xx_bf = round_x_and_square(0)
        quantize_x(0, x_bf, operand(codes, 0))
        quantize_square(0, xx_bf, operand(codes, 1))
        scores(0)
        for i in range(2 * PACK, TILES):
            features(i)
        rewrite_pair(6)
        page_codes = codes_after_scatter(7, 2, I32)
        page_planes(0, page_codes)
        for i in range(PACK, 2 * PACK - 1):
            add_bias(i)

        scatter(8)
        scatter(9)
        for i in range(PACK, 2 * PACK):
            join_by_dma(i)
        begin_page_pair(10)
        end_page_pair(10)
        load_bias(2)
        for i in range(PACK, 2 * PACK):
            store_page(i)
        store_page_codes(0, page_codes)
        scatter(10)
        scatter(11)
        codes = codes_after_scatter(TILES - 1, 4)
        for g in (1, 2):
            round_w2(g)
        add_bias(7)
        x_bf, xx_bf = round_x_and_square(1)
        page_codes = codes_after_scatter(TILES - 2, 2, I32)
        for u in range(2):
            interleave_page(1, u)
        for i in range(2 * PACK, TILES):
            join_rounded(i)
        for i in range(2 * PACK, TILES):
            store_page(i)

        gather(8)
        for u in range(2):
            quantize_page(1, u, page_codes)
        store_page_codes(1, page_codes)
        store_page_scales(0, G - 1)
        gather(9)
        for g in (1, 2):
            quantize_w2(g, operand(codes, g - 1))
        gather(10)
        gather(11)
        quantize_x(1, x_bf, operand(codes, 2))
        quantize_square(1, xx_bf, operand(codes, 3))
        scores(1)
        page_codes = keep.tile([P, T2], I32, name="last_page_codes", align_bytes=64)
        page_planes(2, page_codes)
        store_page_codes(2, page_codes)
        store_page_scales(G - 1, G)
        for i in range(2 * PACK, TILES):
            add_bias(i)
        both = stage_tile([P, 2 * PACK * PICK], BF16)
        x_bf = both[:, 0:PACK * PICK]
        xx_bf = both[:, PACK * PICK:2 * PACK * PICK]
        round_square(2, xx_bf)
        round_x(2, x_bf, nc.vector.tensor_copy)
        codes = keep.tile([P, 2 * PASS], U32, name="last_codes", align_bytes=64)
        quantize_x(2, x_bf, operand(codes, 0))
        quantize_square(2, xx_bf, operand(codes, 1))
        scores(2)
        staged = stage_tile([P, BANKS, PICK], F32)
        for j in range(BANKS):
            store_scores(j, staged, nc.vector.tensor_copy if j % 2 else nc.scalar.copy)
